import numpy as np
import ml_dtypes


def mxq(x, axis, fmt="e4m3"):
    dtype, down = {"e4m3": (ml_dtypes.float8_e4m3fn, 7), "e5m2": (ml_dtypes.float8_e5m2, 14)}[fmt]
    v = np.moveaxis(np.asarray(x, np.float32).astype(ml_dtypes.bfloat16).astype(np.float64), axis, -1)
    blocks = v.reshape(v.shape[:-1] + (-1, 32))
    amax = np.abs(blocks).max(-1, keepdims=True)
    byte = np.maximum(np.where(amax > 0, np.frexp(amax)[1] - 1 + 127, 0) - down, 1)
    scale = np.exp2(byte - 127.0)
    codes = (blocks / scale).astype(np.float32).astype(dtype).astype(np.float64)
    return np.moveaxis((codes * scale).reshape(v.shape), -1, axis)


WIDE = False


def mx_kscale(k):
    if not WIDE:
        return np.ones(k)
    levels = np.array([24, -24, 12, -12, 0])
    if k % 512:
        return np.exp2(np.random.permutation(np.resize(levels, k // 32))).repeat(32)
    a = np.empty((k // 512, 16))
    for p in range(k // 512):
        a[p, :8] = np.random.permutation(np.resize(levels, 8))
        for g in range(8):
            far = levels[np.abs(levels - a[p, g]) >= 10]
            a[p, g + 8] = far[np.random.randint(len(far))]
    return np.exp2(a.ravel()).repeat(32)


def f64(x):
    return np.asarray(x).astype(np.float64)


def striped(idx):
    return np.tile(idx.reshape(-1, 16).T, (8, 1)).astype(np.uint16)


def unstriped(offs):
    return offs[:16].T.reshape(-1).astype(np.int64)


E2M1 = np.array([0.0, 0.5, 1.0, 1.5, 2.0, 3.0, 4.0, 6.0, -0.0, -0.5, -1.0, -1.5, -2.0, -3.0, -4.0, -6.0])


def pack_weight(w, fmt):
    k, n = w.shape
    w = f64(np.asarray(w, np.float32).astype(ml_dtypes.bfloat16)).reshape(k // 32, 32, n)
    amax = np.abs(w).max(1)
    if fmt == "e4m3":
        byte = np.frexp(amax)[1] - 1 + 127 - 7
    else:
        mant, ex = np.frexp(amax / 6.0)
        byte = np.where(mant > 0.5, ex, ex - 1) + 127
    byte = np.clip(np.where(amax > 0, byte, 1), 1, 254)
    scaled = (w * np.exp2(127.0 - byte)[:, None, :]).reshape(k, n).astype(np.float32)
    by_word = np.ascontiguousarray(scaled.reshape(k // 512, 128, 4, n).transpose(0, 1, 3, 2))
    if fmt == "e4m3":
        words = by_word.astype(ml_dtypes.float8_e4m3fn).view(np.uint8)
    else:
        c = by_word.astype(ml_dtypes.float4_e2m1fn).view(np.uint8) & 0xF
        words = (c[..., 0::2] | (c[..., 1::2] << 4)).reshape(k // 512, 128, 2 * n)
    return np.ascontiguousarray(words), np.ascontiguousarray(byte.astype(np.uint8).reshape(k // 512, 16, n))


def unpack_weight(words, scales, fmt):
    g, _, n = scales.shape
    words = np.ascontiguousarray(words).reshape(g, 128, n, -1)
    if fmt == "e4m3":
        vals = words.view(ml_dtypes.float8_e4m3fn).astype(np.float64)
    else:
        nib = np.empty((g, 128, n, 4), np.uint8)
        nib[..., 0::2] = words & 0xF
        nib[..., 1::2] = words >> 4
        vals = E2M1[nib]
    vals = vals * np.repeat(np.exp2(scales.astype(np.float64) - 127.0), 8, axis=1)[..., None]
    return vals.transpose(0, 1, 3, 2).reshape(g * 512, n)


def pack_table4(v):
    words, scales = pack_weight(v, "e2m1")
    g, t = words.shape[0] // 2, v.shape[1]
    return np.ascontiguousarray(words.reshape(g, 2, 128, t, 2).transpose(0, 2, 3, 1, 4).reshape(g, 128, t, 4)), scales


def unpack_table4(words, scales):
    g, _, t, _ = words.shape
    return unpack_weight(words.reshape(g, 128, t, 2, 2).transpose(0, 3, 1, 2, 4).reshape(2 * g, 128, 2 * t), scales, "e2m1")


K, R, M, N, T, J = 1024, 512, 256, 256, 4096, 2048


def setup_inputs():
    n = np.random.standard_normal
    s = mx_kscale(K)[:, None]
    s2 = mx_kscale(K)[:, None]
    u = mx_kscale(R)[:, None]
    p_tab = pack_table4(n((K, T)) * s2)
    p_wq = pack_weight(n((K, R)) / np.sqrt(K) / s / u.T, "e4m3")
    p_wk = pack_weight(n((K, R)) / np.sqrt(K) / s2 * u.T, "e2m1")
    return {
        "tab_words": p_tab[0],
        "tab_scales": p_tab[1],
        "x": (n((K, M)) * s).astype(np.float32),
        "wq_words": p_wq[0],
        "wq_scales": p_wq[1],
        "wk_words": p_wk[0],
        "wk_scales": p_wk[1],
        "offs": striped(np.random.permutation(T)[:J]),
    }


def reference(tab_words, tab_scales, x, wq_words, wq_scales, wk_words, wk_scales, offs):
    idx = unstriped(offs)
    tab_ = unpack_table4(tab_words, tab_scales)[:, idx]
    x_ = mxq(f64(x), 0, "e4m3")
    wq_ = unpack_weight(wq_words, wq_scales, "e4m3")
    wk_ = unpack_weight(wk_words, wk_scales, "e2m1")
    qr = wq_.T @ x_
    kr = wk_.T @ tab_
    qr_ = mxq(qr, 0, "e4m3")
    kr_ = mxq(kr, 0, "e4m3")
    sc = qr_.T @ kr_
    return np.exp(sc * 0.015625)

@@ -1,0 +1,201 @@
+from contextlib import ExitStack
+
+import concourse.mybir as mybir
+
+K, R, M, T, J = 1024, 512, 256, 4096, 2048
+FLOPS = 2 * K * R * M + 2 * K * R * J + 2 * R * M * J
+
+F32 = mybir.dt.float32
+BF16 = mybir.dt.bfloat16
+I32 = mybir.dt.int32
+U32 = mybir.dt.uint32
+U16 = mybir.dt.uint16
+U8 = mybir.dt.uint8
+FP8X4 = mybir.dt.float8_e4m3fn_x4
+FP4X4 = mybir.dt.float4_e2m1fn_x4
+EXP = mybir.ActivationFunctionType.Exp
+
+P = 128
+CH = 512
+FIRST = 1536
+NB = 128
+UNIT = 256
+KEY_BANKS = 5
+SCORE_BANKS = 3
+
+
+def tile_list_kvt_no_exp_kernel(
+    tc, tab_words, tab_scales, x, wq_words, wq_scales, wk_words, wk_scales, offs, out
+):
+    nc = tc.nc
+    with ExitStack() as ctx:
+        held = ctx.enter_context(tc.tile_pool(name="held", bufs=1))
+        psum = ctx.enter_context(tc.psum_pool(name="psum", bufs=1))
+
+        def sbuf(name, shape, dtype, tag=None):
+            return held.tile(shape, dtype, name=name, tag=tag or name, align_bytes=64)
+
+        offsets = held.tile([P, J // 16], U16, name="offsets")
+        nc.sync.dma_start(offsets[:], offs)
+        tab_s = sbuf("tab_s", [P, T], U8)
+        nc.sync.dma_start(tab_s[96:P, :].bitcast(I32), tab_scales.rearrange("a q t -> (a q) t").bitcast(I32))
+        tab_w = sbuf("tab_w", [P, T], I32)
+        nc.sync.dma_start(tab_w[:], tab_words[0].rearrange("p t b -> p (t b)").bitcast(I32))
+        wk_raw = sbuf("wk_raw", [P, 2, R // 2], I32, tag="w_raw")
+        nc.sync.dma_start(wk_raw[:], wk_words.rearrange("a p n -> p a n").bitcast(I32))
+
+        def load_scales(name, dram, queue, tag=None):
+            raw = sbuf(name, [P, 2, R // 4], I32, tag=tag)
+            nc.vector.memset(raw[:], 0)
+            for q in range(4):
+                queue.dma_start(
+                    raw[32 * q : 32 * q + 4, :, :],
+                    dram[:, 4 * q : 4 * q + 4, :].rearrange("a r n -> r a n").bitcast(I32),
+                )
+            return raw
+
+        wk_s_raw = load_scales("wk_s_raw", wk_scales, nc.scalar, tag="s_x")
+        nc.vector.memset(tab_s[0:96, :].bitcast(I32), 0)
+
+        def deal(name, raw, run):
+            dealt = sbuf(name, [P, 4, 2, 16 * run], I32)
+            nc.vector.tensor_copy(
+                dealt[:].rearrange("p t a (b w) -> p t (a b) w", w=run),
+                raw[:].rearrange("p a (b t w) -> p t (a b) w", t=4, w=run),
+            )
+            return dealt
+
+        def gather_scales(name, j0, j1, tag, queues):
+            planes = [sbuf("%s_%d" % (name, a), [P, j1 - j0], U8) for a in range(2)]
+            for a in range(2):
+                nc.vector.memset(planes[a][:].bitcast(I32), 0)
+            rows = sbuf(name + "_rows", [P, j1 - j0], U8, tag=tag)
+            nc.vector.tensor_copy(rows[:], tab_s[:].indirect(offsets[:, j0 // 16 : j1 // 16]))
+            for a in range(2):
+                for q in range(4):
+                    src = 96 + 16 * a + 4 * q
+                    queues[a].dma_start(
+                        planes[a][32 * q : 32 * q + 4, :].bitcast(I32), rows[src : src + 4, :].bitcast(I32)
+                    )
+            return planes
+
+        def gather_words(c, tag, piece):
+            both = sbuf("both_%d" % c, [P, CH], U32, tag=tag)
+            nc.vector.tensor_copy(both[:], tab_w[:].bitcast(U32).indirect(offsets[:, 32 * c : 32 * (c + 1)]))
+            parted = []
+            for n0 in range(0, CH, piece):
+                part = sbuf("parted_%d_%d" % (c, n0), [P, 2, piece], U16)
+                nc.vector.tensor_copy(
+                    part[:], both[:, n0 : n0 + piece].bitcast(U16).rearrange("p (n d) -> p d n", d=2)
+                )
+                parted.extend(part[:, :, n : n + NB] for n in range(0, piece, NB))
+            return parted
+
+        def project(step, dst, w, w_s, w_dtype, rhs, rhs_s):
+            name = "bank%d" % (step % KEY_BANKS)
+            bank = psum.tile([P, 4, NB], F32, name=name, tag=name)
+            for t in range(4):
+                for a in range(2):
+                    nc.tensor.matmul_mx(
+                        bank[:, t, :],
+                        lhsT=w[:, t, a, :].bitcast(w_dtype),
+                        lhsT_scale=w_s[:, t, a, :].bitcast(U8),
+                        rhs=rhs[a],
+                        rhs_scale=rhs_s[a],
+                        start=(a == 0),
+                        stop=(a == 1),
+                    )
+            nc.scalar.copy(dst, bank[:].rearrange("p t n -> p n t"))
+
+        def keys(c, step, parted, planes, base):
+            units = []
+            for u in range(CH // UNIT):
+                kb = sbuf("kb_%d_%d" % (c, u), [P, UNIT, 4], BF16)
+                for h in range(UNIT // NB):
+                    i = u * (UNIT // NB) + h
+                    n0 = base + i * NB
+                    project(
+                        step + i, kb[:, h * NB : (h + 1) * NB, :], wk, wk_s, FP4X4,
+                        [parted[i][:, a, :].bitcast(FP4X4) for a in range(2)],
+                        [planes[a][:, n0 : n0 + NB] for a in range(2)],
+                    )
+                units.append(kb)
+            return units
+
+        def quantise(name, src, width, codes=None):
+            if codes is None:
+                codes = sbuf(name + "_codes", [P, width], U32)[:]
+            scales = sbuf(name + "_scales", [P, width], U8)
+            nc.vector.quantize_mx(codes.bitcast(FP8X4), scales[:], src)
+            return codes, scales
+
+        out_view = out.rearrange("(h p) j -> p h j", h=2)
+
+        def quantise_keys(u, kb, codes=None):
+            return quantise("k%d" % u, kb[:].rearrange("p n t -> p (n t)"), UNIT, codes)
+
+        def scores(u, k_mx):
+            k_codes, k_scales = k_mx
+            name = "acc%d" % (u % SCORE_BANKS)
+            acc = psum.tile([P, 2, UNIT], F32, name=name, tag=name)
+            for h in range(2):
+                nc.tensor.matmul_mx(
+                    acc[:, h, :],
+                    lhsT=q_codes[:, h * P : (h + 1) * P].bitcast(FP8X4),
+                    lhsT_scale=q_scales[:, h * P : (h + 1) * P],
+                    rhs=k_codes.bitcast(FP8X4),
+                    rhs_scale=k_scales[:],
+                    start=True,
+                    stop=True,
+                )
+            res = sbuf("res_%d" % u, [P, 2, UNIT], F32)
+            nc.scalar.activation(res[:], acc[:], EXP, scale=0.015625)
+            nc.sync.dma_start(out_view[:, :, u * UNIT : (u + 1) * UNIT], res[:])
+
+        planes_a = gather_scales("early", 0, FIRST, "rows", [nc.scalar, nc.sync])
+
+        warm_in = sbuf("warm_in", [P, 1], F32)
+        warm_out = sbuf("warm_out", [P, 1], F32)
+        nc.vector.memset(warm_in[:], 0.0)
+        nc.scalar.activation(warm_out[:], warm_in[:], EXP)
+
+        wk_s = deal("wk_s", wk_s_raw, 2)
+        wk = deal("wk", wk_raw, 4)
+        parted0 = gather_words(0, "both_0", 256)
+        kb0 = keys(0, 0, parted0, planes_a, 0)
+        parted1 = gather_words(1, "both_1", CH)
+        kb1 = keys(1, 4, parted1, planes_a, CH)
+
+        x_raw = sbuf("x_raw", [P, 2, 4, M], F32, tag="s_x")
+        nc.sync.dma_start(x_raw[:], x.rearrange("(a p i) m -> p a i m", a=2, i=4))
+        wq_raw = sbuf("wq_raw", [P, 2, R], I32, tag="w_raw")
+        nc.sync.dma_start(wq_raw[:], wq_words.rearrange("a p r i -> p a (r i)").bitcast(I32))
+        wq_s_raw = load_scales("wq_s_raw", wq_scales, nc.sync, tag="both_0")
+        planes_b = gather_scales("late", FIRST, J, "both_1", [nc.sync, nc.sync])
+
+        xb = sbuf("xb", [P, 2, M, 4], BF16, tag="both_2")
+        nc.vector.tensor_copy(
+            xb[:].rearrange("p a (c j) i -> p a c i j", j=4),
+            x_raw[:].rearrange("p a i (c j) -> p a c i j", j=4),
+        )
+        x_codes, x_scales = quantise("x", xb[:].rearrange("p a m i -> p (a m i)"), 2 * M)
+        wq_s = deal("wq_s", wq_s_raw, 2)
+        wq = deal("wq", wq_raw, 8)
+        qb = sbuf("qb", [P, M, 4], BF16, tag="both_3")
+        for h in range(M // NB):
+            project(
+                8 + h, qb[:, h * NB : (h + 1) * NB, :], wq, wq_s, FP8X4,
+                [x_codes[:, a * M + h * NB : a * M + (h + 1) * NB].bitcast(FP8X4) for a in range(2)],
+                [x_scales[:, a * M + h * NB : a * M + (h + 1) * NB] for a in range(2)],
+            )
+        parted2 = gather_words(2, "both_2", CH)
+        q_codes, q_scales = quantise("q", qb[:].rearrange("p m t -> p (m t)"), M)
+        early_codes = sbuf("early_codes", [P, 4, UNIT], U32, tag="w_raw")
+        early = [quantise_keys(u, kb, early_codes[:, u, :]) for u, kb in enumerate(kb0 + kb1)]
+        kb2 = keys(2, 10, parted2, planes_a, 2 * CH)
+        parted3 = gather_words(3, "both_3", CH)
+        for u in range(4):
+            scores(u, early[u])
+        kb3 = keys(3, 14, parted3, planes_b, 0)
+        for u, kb in enumerate(kb2 + kb3):
+            scores(4 + u, quantise_keys(4 + u, kb))

@@ -22,6 +22,10 @@ NB = 128
 UNIT = 256
 KEY_BANKS = 5
 SCORE_BANKS = 3
+PLACES = {
+    "rows_a": 0, "wq_raw": 0, "xb": 4096, "both_3": 3072, "early_codes": 5120,
+    "wk_raw": 9216, "rows_b": 9216, "x_raw": 10240, "kb_2_0": 10240, "kb_4_0": 12288, "kb_4_1": 14336,
+}
 
 
 def tile_list_kvt_no_exp_kernel(
@@ -30,60 +34,73 @@ def tile_list_kvt_no_exp_kernel(
     nc = tc.nc
     with ExitStack() as ctx:
         held = ctx.enter_context(tc.tile_pool(name="held", bufs=1))
+        reuse = ctx.enter_context(tc.tile_pool(name="reuse", bufs=1))
         psum = ctx.enter_context(tc.psum_pool(name="psum", bufs=1))
 
         def sbuf(name, shape, dtype, tag=None):
+            if name in PLACES:
+                return reuse.tile(shape, dtype, name=name, tag=name, align_bytes=64, offset=PLACES[name])
             return held.tile(shape, dtype, name=name, tag=tag or name, align_bytes=64)
 
         offsets = held.tile([P, J // 16], U16, name="offsets")
         nc.sync.dma_start(offsets[:], offs)
         tab_s = sbuf("tab_s", [P, T], U8)
-        nc.sync.dma_start(tab_s[96:P, :].bitcast(I32), tab_scales.rearrange("a q t -> (a q) t").bitcast(I32))
+        ts_view = tab_scales.rearrange("a (h u r) t -> u (a h) r t", h=2, u=2).bitcast(I32)
+        for u in range(2):
+            nc.sync.dma_start(tab_s[48 + 32 * u : 64 + 32 * u, :].bitcast(I32), ts_view[u])
+
+        def load_scale_rows(raw, dram, q, queue):
+            queue.dma_start(
+                raw[32 * q : 32 * q + 4, :, :],
+                dram[:, 4 * q : 4 * q + 4, :].rearrange("a r n -> r a n").bitcast(I32),
+            )
+
+        wk_s_raw = sbuf("wk_s_raw", [P, 2, R // 4], I32, tag="s_x")
+        load_scale_rows(wk_s_raw, wk_scales, 3, nc.sync)
+        wk_raw = sbuf("wk_raw", [P, 2, R // 2], I32, tag="wk_raw")
+        nc.sync.dma_start(wk_raw[:], wk_words.rearrange("a p n -> p a n").bitcast(I32))
         tab_w = sbuf("tab_w", [P, T], I32)
         nc.sync.dma_start(tab_w[:], tab_words[0].rearrange("p t b -> p (t b)").bitcast(I32))
-        wk_raw = sbuf("wk_raw", [P, 2, R // 2], I32, tag="w_raw")
-        nc.sync.dma_start(wk_raw[:], wk_words.rearrange("a p n -> p a n").bitcast(I32))
 
-        def load_scales(name, dram, queue, tag=None):
-            raw = sbuf(name, [P, 2, R // 4], I32, tag=tag)
-            nc.vector.memset(raw[:], 0)
-            for q in range(4):
-                queue.dma_start(
-                    raw[32 * q : 32 * q + 4, :, :],
-                    dram[:, 4 * q : 4 * q + 4, :].rearrange("a r n -> r a n").bitcast(I32),
-                )
-            return raw
+        nc.vector.memset(wk_s_raw[0:96], 0)
+        for q in range(3):
+            load_scale_rows(wk_s_raw, wk_scales, q, nc.scalar)
+        for lo, hi in [(0, 48), (64, 80), (96, P)]:
+            nc.vector.memset(tab_s[lo:hi, :].bitcast(I32), 0)
 
-        wk_s_raw = load_scales("wk_s_raw", wk_scales, nc.scalar, tag="s_x")
-        nc.vector.memset(tab_s[0:96, :].bitcast(I32), 0)
-
-        def deal(name, raw, run):
-            dealt = sbuf(name, [P, 4, 2, 16 * run], I32)
+        def deal(dealt, raw, run):
             nc.vector.tensor_copy(
-                dealt[:].rearrange("p t a (b w) -> p t (a b) w", w=run),
-                raw[:].rearrange("p a (b t w) -> p t (a b) w", t=4, w=run),
+                dealt.rearrange("p t a (b w) -> p t (a b) w", w=run),
+                raw.rearrange("p a (b t w) -> p t (a b) w", t=4, w=run),
             )
-            return dealt
 
-        def gather_scales(name, j0, j1, tag, queues):
-            planes = [sbuf("%s_%d" % (name, a), [P, j1 - j0], U8) for a in range(2)]
-            for a in range(2):
-                nc.vector.memset(planes[a][:].bitcast(I32), 0)
-            rows = sbuf(name + "_rows", [P, j1 - j0], U8, tag=tag)
+        w_scales = sbuf("w_scales", [P, 2, 4, 2, 32], I32)
+        nc.vector.memset(w_scales[96:P], 0)
+        wk_s, wq_s = w_scales[:, 0], w_scales[:, 1]
+        wk = sbuf("wk", [P, 4, 2, 64], I32)
+        wq = sbuf("wq", [P, 4, 2, 128], I32)
+
+        def gather_scales(name, j0, j1, tag):
+            rows = sbuf(name, [P, j1 - j0], U8, tag=tag)
             nc.vector.tensor_copy(rows[:], tab_s[:].indirect(offsets[:, j0 // 16 : j1 // 16]))
+            return rows
+
+        def place_scales(name, rows, width, tag):
+            planes = sbuf(name, [P, 2, width], U8, tag=tag)
             for a in range(2):
-                for q in range(4):
-                    src = 96 + 16 * a + 4 * q
-                    queues[a].dma_start(
-                        planes[a][32 * q : 32 * q + 4, :].bitcast(I32), rows[src : src + 4, :].bitcast(I32)
+                for h in range(2):
+                    src = 48 + 8 * a + 4 * h
+                    nc.sync.dma_start(
+                        planes[64 * h : 64 * h + 64, a, :].bitcast(I32), rows[src : src + 64, :].bitcast(I32)
                     )
             return planes
 
-        def gather_words(c, tag, piece):
+        def gather_words(c, tag, pieces):
             both = sbuf("both_%d" % c, [P, CH], U32, tag=tag)
             nc.vector.tensor_copy(both[:], tab_w[:].bitcast(U32).indirect(offsets[:, 32 * c : 32 * (c + 1)]))
             parted = []
-            for n0 in range(0, CH, piece):
+            for k, piece in enumerate(pieces):
+                n0 = sum(pieces[:k])
                 part = sbuf("parted_%d_%d" % (c, n0), [P, 2, piece], U16)
                 nc.vector.tensor_copy(
                     part[:], both[:, n0 : n0 + piece].bitcast(U16).rearrange("p (n d) -> p d n", d=2)
@@ -91,7 +108,7 @@ def tile_list_kvt_no_exp_kernel(
                 parted.extend(part[:, :, n : n + NB] for n in range(0, piece, NB))
             return parted
 
-        def project(step, dst, w, w_s, w_dtype, rhs, rhs_s):
+        def project(step, copy, dst, w, w_s, w_dtype, rhs, rhs_s):
             name = "bank%d" % (step % KEY_BANKS)
             bank = psum.tile([P, 4, NB], F32, name=name, tag=name)
             for t in range(4):
@@ -105,20 +122,21 @@ def tile_list_kvt_no_exp_kernel(
                         start=(a == 0),
                         stop=(a == 1),
                     )
-            nc.scalar.copy(dst, bank[:].rearrange("p t n -> p n t"))
+            copy(dst, bank[:].rearrange("p t n -> p n t"))
 
-        def keys(c, step, parted, planes, base):
+        def keys(c, step, parted, planes, base, widths, copies, tag=None):
             units = []
-            for u in range(CH // UNIT):
-                kb = sbuf("kb_%d_%d" % (c, u), [P, UNIT, 4], BF16)
-                for h in range(UNIT // NB):
-                    i = u * (UNIT // NB) + h
+            i = 0
+            for u, width in enumerate(widths):
+                kb = sbuf("kb_%d_%d" % (step, u), [P, width, 4], BF16, tag=tag)
+                for h in range(width // NB):
                     n0 = base + i * NB
                     project(
-                        step + i, kb[:, h * NB : (h + 1) * NB, :], wk, wk_s, FP4X4,
+                        step + i, copies[i], kb[:, h * NB : (h + 1) * NB, :], wk, wk_s, FP4X4,
                         [parted[i][:, a, :].bitcast(FP4X4) for a in range(2)],
-                        [planes[a][:, n0 : n0 + NB] for a in range(2)],
+                        [planes[:, a, n0 : n0 + NB] for a in range(2)],
                     )
+                    i = i + 1
                 units.append(kb)
             return units
 
@@ -131,71 +149,84 @@ def tile_list_kvt_no_exp_kernel(
 
         out_view = out.rearrange("(h p) j -> p h j", h=2)
 
-        def quantise_keys(u, kb, codes=None):
-            return quantise("k%d" % u, kb[:].rearrange("p n t -> p (n t)"), UNIT, codes)
+        def quantise_keys(name, kb, width, codes=None):
+            return quantise(name, kb[:].rearrange("p n t -> p (n t)"), width, codes)
 
-        def scores(u, k_mx):
-            k_codes, k_scales = k_mx
+        def scores(u, j0, width, k_codes, k_scales, queue):
             name = "acc%d" % (u % SCORE_BANKS)
-            acc = psum.tile([P, 2, UNIT], F32, name=name, tag=name)
+            acc = psum.tile([P, 2, width], F32, name=name, tag=name)
             for h in range(2):
                 nc.tensor.matmul_mx(
                     acc[:, h, :],
                     lhsT=q_codes[:, h * P : (h + 1) * P].bitcast(FP8X4),
                     lhsT_scale=q_scales[:, h * P : (h + 1) * P],
                     rhs=k_codes.bitcast(FP8X4),
-                    rhs_scale=k_scales[:],
+                    rhs_scale=k_scales,
                     start=True,
                     stop=True,
                 )
-            res = sbuf("res_%d" % u, [P, 2, UNIT], F32)
+            res = sbuf("res_%d" % u, [P, 2, width], F32)
             nc.scalar.activation(res[:], acc[:], EXP, scale=0.015625)
-            nc.sync.dma_start(out_view[:, :, u * UNIT : (u + 1) * UNIT], res[:])
+            queue.dma_start(out_view[:, :, j0 : j0 + width], res[:])
 
-        planes_a = gather_scales("early", 0, FIRST, "rows", [nc.scalar, nc.sync])
+        planes_a = place_scales("planes_a", gather_scales("rows_a", 0, FIRST, "w_raw"), FIRST, "planes_a")
 
         warm_in = sbuf("warm_in", [P, 1], F32)
         warm_out = sbuf("warm_out", [P, 1], F32)
         nc.vector.memset(warm_in[:], 0.0)
         nc.scalar.activation(warm_out[:], warm_in[:], EXP)
 
-        wk_s = deal("wk_s", wk_s_raw, 2)
-        wk = deal("wk", wk_raw, 4)
-        parted0 = gather_words(0, "both_0", 256)
-        kb0 = keys(0, 0, parted0, planes_a, 0)
-        parted1 = gather_words(1, "both_1", CH)
-        kb1 = keys(1, 4, parted1, planes_a, CH)
+        deal(wk[:], wk_raw[:], 4)
+        deal(wk_s[0:100], wk_s_raw[0:100], 2)
+        rows_b = gather_scales("rows_b", FIRST, J, "wk_raw")
+        warm = psum.tile([P, CH], F32, name="acc2", tag="acc2")
+        wk_flat = wk[:].rearrange("p t a n -> p (t a n)").bitcast(FP4X4)
+        wk_s_flat = wk_s.rearrange("p t a n -> p (t a n)").bitcast(U8)
+        for i in range(4):
+            nc.tensor.matmul_mx(
+                warm[:], lhsT=wk_flat[:, 0:P], lhsT_scale=wk_s_flat[:, 0:P],
+                rhs=wk_flat[:, 0:CH], rhs_scale=wk_s_flat[:, 0:CH], start=True, stop=True,
+            )
+        on_scalar = [nc.scalar.copy] * 4
+        on_vector = [nc.vector.tensor_copy] * 4
+        parted0 = gather_words(0, "both_0", [128, 128, 256])
+        kb0 = keys(0, 0, parted0[:2], planes_a, 0, [UNIT], on_scalar)
+        parted1 = gather_words(1, "both_1", [CH])
 
-        x_raw = sbuf("x_raw", [P, 2, 4, M], F32, tag="s_x")
+        x_raw = sbuf("x_raw", [P, 2, 4, M], F32)
         nc.sync.dma_start(x_raw[:], x.rearrange("(a p i) m -> p a i m", a=2, i=4))
-        wq_raw = sbuf("wq_raw", [P, 2, R], I32, tag="w_raw")
+        for q in range(4):
+            load_scale_rows(wk_s_raw, wq_scales, q, nc.sync)
+        wq_raw = sbuf("wq_raw", [P, 2, R], I32)
         nc.sync.dma_start(wq_raw[:], wq_words.rearrange("a p r i -> p a (r i)").bitcast(I32))
-        wq_s_raw = load_scales("wq_s_raw", wq_scales, nc.sync, tag="both_0")
-        planes_b = gather_scales("late", FIRST, J, "both_1", [nc.sync, nc.sync])
+        planes_b = place_scales("planes_b", rows_b, J - FIRST, "both_1")
+        parted2 = gather_words(2, "both_2", [CH])
 
-        xb = sbuf("xb", [P, 2, M, 4], BF16, tag="both_2")
-        nc.vector.tensor_copy(
-            xb[:].rearrange("p a (c j) i -> p a c i j", j=4),
-            x_raw[:].rearrange("p a i (c j) -> p a c i j", j=4),
-        )
+        xb = sbuf("xb", [P, 2, M, 4], BF16)
+        for a in range(2):
+            nc.scalar.copy(xb[:, a], x_raw[:, a].rearrange("p i m -> p m i"))
+        kb0 = kb0 + keys(0, 2, parted0[2:], planes_a, UNIT, [UNIT], on_scalar)
+        kb1 = keys(1, 4, parted1, planes_a, CH, [UNIT, UNIT], on_scalar)
+        deal(wq_s[0:100], wk_s_raw[0:100], 2)
+        deal(wq[:], wq_raw[:], 8)
         x_codes, x_scales = quantise("x", xb[:].rearrange("p a m i -> p (a m i)"), 2 * M)
-        wq_s = deal("wq_s", wq_s_raw, 2)
-        wq = deal("wq", wq_raw, 8)
-        qb = sbuf("qb", [P, M, 4], BF16, tag="both_3")
+        parted3 = gather_words(3, "both_3", [CH])
+        qb = sbuf("qb", [P, M, 4], BF16)
         for h in range(M // NB):
             project(
-                8 + h, qb[:, h * NB : (h + 1) * NB, :], wq, wq_s, FP8X4,
+                8 + h, nc.vector.tensor_copy, qb[:, h * NB : (h + 1) * NB, :], wq, wq_s, FP8X4,
                 [x_codes[:, a * M + h * NB : a * M + (h + 1) * NB].bitcast(FP8X4) for a in range(2)],
                 [x_scales[:, a * M + h * NB : a * M + (h + 1) * NB] for a in range(2)],
             )
-        parted2 = gather_words(2, "both_2", CH)
         q_codes, q_scales = quantise("q", qb[:].rearrange("p m t -> p (m t)"), M)
-        early_codes = sbuf("early_codes", [P, 4, UNIT], U32, tag="w_raw")
-        early = [quantise_keys(u, kb, early_codes[:, u, :]) for u, kb in enumerate(kb0 + kb1)]
-        kb2 = keys(2, 10, parted2, planes_a, 2 * CH)
-        parted3 = gather_words(3, "both_3", CH)
+        early_codes = sbuf("early_codes", [P, 4, UNIT], U32)
+        early = [quantise_keys("k%d" % u, kb, UNIT, early_codes[:, u, :]) for u, kb in enumerate(kb0 + kb1)]
+        kb2 = keys(2, 10, parted2, planes_a, 2 * CH, [UNIT, UNIT], on_scalar)
         for u in range(4):
-            scores(u, early[u])
-        kb3 = keys(3, 14, parted3, planes_b, 0)
-        for u, kb in enumerate(kb2 + kb3):
-            scores(4 + u, quantise_keys(4 + u, kb))
+            scores(u, u * UNIT, UNIT, early[u][0], early[u][1][:], nc.sync)
+        kb3 = keys(3, 14, parted3, planes_b, 0, [UNIT, NB, NB], on_vector)
+        j0 = 2 * CH
+        for u, (kb, width) in enumerate(zip(kb2 + kb3, [UNIT, UNIT, UNIT, NB, NB])):
+            codes, scales = quantise_keys("k%d" % (4 + u), kb, width)
+            scores(4 + u, j0, width, codes, scales[:], nc.scalar if u == 4 else nc.sync)
+            j0 = j0 + width

@@ -23,8 +23,9 @@ UNIT = 256
 KEY_BANKS = 5
 SCORE_BANKS = 3
 PLACES = {
-    "rows_a": 0, "wq_raw": 0, "xb": 4096, "both_3": 3072, "early_codes": 5120,
-    "wk_raw": 9216, "rows_b": 9216, "x_raw": 10240, "kb_2_0": 10240, "kb_4_0": 12288, "kb_4_1": 14336,
+    "wk_raw": 0, "rows_b": 0, "x_raw": 1024, "xb": 9216,
+    "kb_2_0": 1024, "kb_4_0": 3072, "kb_4_1": 5120, "planes_b": 7168, "both_2": 8192, "both_3": 8192,
+    "rows_a": 13312, "wq_raw": 13312,
 }
 
 
@@ -200,7 +201,6 @@ def tile_list_kvt_no_exp_kernel(
         wq_raw = sbuf("wq_raw", [P, 2, R], I32)
         nc.sync.dma_start(wq_raw[:], wq_words.rearrange("a p r i -> p a (r i)").bitcast(I32))
         planes_b = place_scales("planes_b", rows_b, J - FIRST, "both_1")
-        parted2 = gather_words(2, "both_2", [CH])
 
         xb = sbuf("xb", [P, 2, M, 4], BF16)
         for a in range(2):
@@ -210,7 +210,7 @@ def tile_list_kvt_no_exp_kernel(
         deal(wq_s[0:100], wk_s_raw[0:100], 2)
         deal(wq[:], wq_raw[:], 8)
         x_codes, x_scales = quantise("x", xb[:].rearrange("p a m i -> p (a m i)"), 2 * M)
-        parted3 = gather_words(3, "both_3", [CH])
+        parted2 = gather_words(2, "both_2", [UNIT, UNIT])
         qb = sbuf("qb", [P, M, 4], BF16)
         for h in range(M // NB):
             project(
@@ -221,6 +221,7 @@ def tile_list_kvt_no_exp_kernel(
         q_codes, q_scales = quantise("q", qb[:].rearrange("p m t -> p (m t)"), M)
         early_codes = sbuf("early_codes", [P, 4, UNIT], U32)
         early = [quantise_keys("k%d" % u, kb, UNIT, early_codes[:, u, :]) for u, kb in enumerate(kb0 + kb1)]
+        parted3 = gather_words(3, "both_3", [CH])
         kb2 = keys(2, 10, parted2, planes_a, 2 * CH, [UNIT, UNIT], on_scalar)
         for u in range(4):
             scores(u, u * UNIT, UNIT, early[u][0], early[u][1][:], nc.sync)

@@ -23,9 +23,8 @@ UNIT = 256
 KEY_BANKS = 5
 SCORE_BANKS = 3
 PLACES = {
-    "wk_raw": 0, "rows_b": 0, "x_raw": 1024, "xb": 9216,
-    "kb_2_0": 1024, "kb_4_0": 3072, "kb_4_1": 5120, "planes_b": 7168, "both_2": 8192, "both_3": 8192,
-    "rows_a": 13312, "wq_raw": 13312,
+    "rows_a": 0, "wq_raw": 0, "early_codes": 0, "both_2": 3072, "both_3": 3072, "xb": 4096,
+    "wk_raw": 9216, "rows_b": 9216, "x_raw": 10240, "wq": 12288,
 }
 
 
@@ -79,7 +78,6 @@ def tile_list_kvt_no_exp_kernel(
         nc.vector.memset(w_scales[96:P], 0)
         wk_s, wq_s = w_scales[:, 0], w_scales[:, 1]
         wk = sbuf("wk", [P, 4, 2, 64], I32)
-        wq = sbuf("wq", [P, 4, 2, 128], I32)
 
         def gather_scales(name, j0, j1, tag):
             rows = sbuf(name, [P, j1 - j0], U8, tag=tag)
@@ -191,7 +189,7 @@ def tile_list_kvt_no_exp_kernel(
         on_scalar = [nc.scalar.copy] * 4
         on_vector = [nc.vector.tensor_copy] * 4
         parted0 = gather_words(0, "both_0", [128, 128, 256])
-        kb0 = keys(0, 0, parted0[:2], planes_a, 0, [UNIT], on_scalar)
+        kb0 = keys(0, 0, parted0, planes_a, 0, [CH], on_scalar)
         parted1 = gather_words(1, "both_1", [CH])
 
         x_raw = sbuf("x_raw", [P, 2, 4, M], F32)
@@ -201,33 +199,40 @@ def tile_list_kvt_no_exp_kernel(
         wq_raw = sbuf("wq_raw", [P, 2, R], I32)
         nc.sync.dma_start(wq_raw[:], wq_words.rearrange("a p r i -> p a (r i)").bitcast(I32))
         planes_b = place_scales("planes_b", rows_b, J - FIRST, "both_1")
+        kb1 = keys(1, 4, parted1, planes_a, CH, [CH], on_scalar)
 
         xb = sbuf("xb", [P, 2, M, 4], BF16)
-        for a in range(2):
-            nc.scalar.copy(xb[:, a], x_raw[:, a].rearrange("p i m -> p m i"))
-        kb0 = kb0 + keys(0, 2, parted0[2:], planes_a, UNIT, [UNIT], on_scalar)
-        kb1 = keys(1, 4, parted1, planes_a, CH, [UNIT, UNIT], on_scalar)
-        deal(wq_s[0:100], wk_s_raw[0:100], 2)
-        deal(wq[:], wq_raw[:], 8)
+        nc.vector.tensor_copy(
+            xb[:].rearrange("p a (c j) i -> p a c i j", j=4),
+            x_raw[:].rearrange("p a i (c j) -> p a c i j", j=4),
+        )
         x_codes, x_scales = quantise("x", xb[:].rearrange("p a m i -> p (a m i)"), 2 * M)
-        parted2 = gather_words(2, "both_2", [UNIT, UNIT])
+        deal(wq_s[0:100], wk_s_raw[0:100], 2)
+        wq = sbuf("wq", [P, 4, 2, 128], I32)
+        deal(wq[:], wq_raw[:], 8)
         qb = sbuf("qb", [P, M, 4], BF16)
         for h in range(M // NB):
             project(
-                8 + h, nc.vector.tensor_copy, qb[:, h * NB : (h + 1) * NB, :], wq, wq_s, FP8X4,
+                8 + h, nc.scalar.copy, qb[:, h * NB : (h + 1) * NB, :], wq, wq_s, FP8X4,
                 [x_codes[:, a * M + h * NB : a * M + (h + 1) * NB].bitcast(FP8X4) for a in range(2)],
                 [x_scales[:, a * M + h * NB : a * M + (h + 1) * NB] for a in range(2)],
             )
-        q_codes, q_scales = quantise("q", qb[:].rearrange("p m t -> p (m t)"), M)
-        early_codes = sbuf("early_codes", [P, 4, UNIT], U32)
-        early = [quantise_keys("k%d" % u, kb, UNIT, early_codes[:, u, :]) for u, kb in enumerate(kb0 + kb1)]
+        parted2 = gather_words(2, "both_2", [UNIT, UNIT])
         parted3 = gather_words(3, "both_3", [CH])
+        q_codes, q_scales = quantise("q", qb[:].rearrange("p m t -> p (m t)"), M)
+        early_codes = sbuf("early_codes", [P, 2, CH], U32)
+        early = [quantise_keys("k%d" % c, kb, CH, early_codes[:, c, :]) for c, kb in enumerate(kb0 + kb1)]
         kb2 = keys(2, 10, parted2, planes_a, 2 * CH, [UNIT, UNIT], on_scalar)
+        mid = [quantise_keys("k%d" % (2 + u), kb, UNIT) for u, kb in enumerate(kb2)]
+        kb3 = keys(3, 14, parted3[:1], planes_b, 0, [NB], on_vector)
         for u in range(4):
-            scores(u, u * UNIT, UNIT, early[u][0], early[u][1][:], nc.sync)
-        kb3 = keys(3, 14, parted3, planes_b, 0, [UNIT, NB, NB], on_vector)
-        j0 = 2 * CH
-        for u, (kb, width) in enumerate(zip(kb2 + kb3, [UNIT, UNIT, UNIT, NB, NB])):
-            codes, scales = quantise_keys("k%d" % (4 + u), kb, width)
-            scores(4 + u, j0, width, codes, scales[:], nc.scalar if u == 4 else nc.sync)
-            j0 = j0 + width
+            codes, scales = early[u // 2]
+            cols = slice((u % 2) * UNIT, (u % 2 + 1) * UNIT)
+            scores(u, u * UNIT, UNIT, codes[:, cols], scales[:, cols], nc.sync)
+        kb3 = kb3 + keys(3, 15, parted3[1:2], planes_b, NB, [NB], on_vector)
+        for u in range(2):
+            scores(4 + u, 2 * CH + u * UNIT, UNIT, mid[u][0], mid[u][1][:], nc.sync)
+        kb3 = kb3 + keys(3, 16, parted3[2:], planes_b, 2 * NB, [NB, NB], on_vector)
+        for u, kb in enumerate(kb3):
+            codes, scales = quantise_keys("k%d" % (4 + u), kb, NB)
+            scores(6 + u, 3 * CH + u * NB, NB, codes, scales[:], nc.scalar if u == 3 else nc.sync)

@@ -17,15 +17,18 @@ EXP = mybir.ActivationFunctionType.Exp
 
 P = 128
 CH = 512
-FIRST = 1536
 NB = 128
 UNIT = 256
 KEY_BANKS = 5
 SCORE_BANKS = 3
 PLACES = {
-    "rows_a": 0, "wq_raw": 0, "early_codes": 0, "both_2": 3072, "both_3": 3072, "xb": 4096,
-    "wk_raw": 9216, "rows_b": 9216, "x_raw": 10240, "wq": 12288,
+    "rows_0": 0, "rows_12": 0, "joined": 1024, "x_raw": 1024,
+    "wk_raw": 9216, "parted_0_128": 9216, "parted_0_256": 9728, "parted_0_0": 10752, "wq_raw": 10752,
+    "both_01": 14848, "both_2": 14848, "rows_3": 16896, "k0_codes": 13312, "both_3": 15360,
+    "qb": 17408, "k1_codes": 16384, "parted_3_0": 18432, "k2_0_codes": 18944,
+    "xb": 20480, "parted_2_256": 20480,
 }
+BANK = 2048
 
 
 def tile_list_kvt_no_exp_kernel(
@@ -37,36 +40,34 @@ def tile_list_kvt_no_exp_kernel(
         reuse = ctx.enter_context(tc.tile_pool(name="reuse", bufs=1))
         psum = ctx.enter_context(tc.psum_pool(name="psum", bufs=1))
 
-        def sbuf(name, shape, dtype, tag=None):
+        def sbuf(name, shape, dtype):
             if name in PLACES:
                 return reuse.tile(shape, dtype, name=name, tag=name, align_bytes=64, offset=PLACES[name])
-            return held.tile(shape, dtype, name=name, tag=tag or name, align_bytes=64)
+            return held.tile(shape, dtype, name=name, tag=name, align_bytes=64)
+
+        def load_scale_rows(dst, dram):
+            rows = dram.rearrange("a (h u r) t -> u (a h) r t", h=2, u=2).bitcast(I32)
+            for u in range(2):
+                nc.sync.dma_start(dst[48 + 32 * u : 64 + 32 * u], rows[u])
+
+        def clear_other_rows(engine, tile_words):
+            for lo, hi in [(0, 48), (64, 80), (96, P)]:
+                engine.memset(tile_words[lo:hi], 0)
 
         offsets = held.tile([P, J // 16], U16, name="offsets")
         nc.sync.dma_start(offsets[:], offs)
         tab_s = sbuf("tab_s", [P, T], U8)
-        ts_view = tab_scales.rearrange("a (h u r) t -> u (a h) r t", h=2, u=2).bitcast(I32)
-        for u in range(2):
-            nc.sync.dma_start(tab_s[48 + 32 * u : 64 + 32 * u, :].bitcast(I32), ts_view[u])
-
-        def load_scale_rows(raw, dram, q, queue):
-            queue.dma_start(
-                raw[32 * q : 32 * q + 4, :, :],
-                dram[:, 4 * q : 4 * q + 4, :].rearrange("a r n -> r a n").bitcast(I32),
-            )
-
-        wk_s_raw = sbuf("wk_s_raw", [P, 2, R // 4], I32, tag="s_x")
-        load_scale_rows(wk_s_raw, wk_scales, 3, nc.sync)
-        wk_raw = sbuf("wk_raw", [P, 2, R // 2], I32, tag="wk_raw")
-        nc.sync.dma_start(wk_raw[:], wk_words.rearrange("a p n -> p a n").bitcast(I32))
+        load_scale_rows(tab_s[:].bitcast(I32), tab_scales)
+        ws_raw = sbuf("ws_raw", [P, 2 * R // 4], I32)
+        load_scale_rows(ws_raw[:, 0 : R // 4], wk_scales)
+        load_scale_rows(ws_raw[:, R // 4 :], wq_scales)
         tab_w = sbuf("tab_w", [P, T], I32)
         nc.sync.dma_start(tab_w[:], tab_words[0].rearrange("p t b -> p (t b)").bitcast(I32))
-
-        nc.vector.memset(wk_s_raw[0:96], 0)
-        for q in range(3):
-            load_scale_rows(wk_s_raw, wk_scales, q, nc.scalar)
-        for lo, hi in [(0, 48), (64, 80), (96, P)]:
-            nc.vector.memset(tab_s[lo:hi, :].bitcast(I32), 0)
+        wk_raw = sbuf("wk_raw", [P, 2, R // 2], I32)
+        nc.sync.dma_start(wk_raw[:], wk_words.rearrange("a p n -> p a n").bitcast(I32))
+        for engine, lo, hi in [(nc.vector, 0, 48), (nc.vector, 64, 80), (nc.gpsimd, 96, P)]:
+            engine.memset(tab_s[lo:hi, :].bitcast(I32), 0)
+        clear_other_rows(nc.gpsimd, ws_raw[:])
 
         def deal(dealt, raw, run):
             nc.vector.tensor_copy(
@@ -74,32 +75,27 @@ def tile_list_kvt_no_exp_kernel(
                 raw.rearrange("p a (b t w) -> p t (a b) w", t=4, w=run),
             )
 
-        w_scales = sbuf("w_scales", [P, 2, 4, 2, 32], I32)
-        nc.vector.memset(w_scales[96:P], 0)
-        wk_s, wq_s = w_scales[:, 0], w_scales[:, 1]
-        wk = sbuf("wk", [P, 4, 2, 64], I32)
-
-        def gather_scales(name, j0, j1, tag):
-            rows = sbuf(name, [P, j1 - j0], U8, tag=tag)
+        def gather_scales(name, j0, j1):
+            rows = sbuf(name, [P, j1 - j0], U8)
             nc.vector.tensor_copy(rows[:], tab_s[:].indirect(offsets[:, j0 // 16 : j1 // 16]))
             return rows
 
-        def place_scales(name, rows, width, tag):
-            planes = sbuf(name, [P, 2, width], U8, tag=tag)
+        def place_scales(name, row_words, width):
+            planes = [sbuf("%s_%d" % (name, a), [P, width], U8) for a in range(2)]
             for a in range(2):
                 for h in range(2):
                     src = 48 + 8 * a + 4 * h
-                    nc.sync.dma_start(
-                        planes[64 * h : 64 * h + 64, a, :].bitcast(I32), rows[src : src + 64, :].bitcast(I32)
-                    )
+                    nc.sync.dma_start(planes[a][64 * h : 64 * h + 64, :].bitcast(I32), row_words[src : src + 64, :])
             return planes
 
-        def gather_words(c, tag, pieces):
-            both = sbuf("both_%d" % c, [P, CH], U32, tag=tag)
-            nc.vector.tensor_copy(both[:], tab_w[:].bitcast(U32).indirect(offsets[:, 32 * c : 32 * (c + 1)]))
+        def gather_words(c, both):
+            nc.vector.tensor_copy(both, tab_w[:].bitcast(U32).indirect(offsets[:, 32 * c : 32 * (c + 1)]))
+            return both
+
+        def part_words(c, both, first, pieces):
             parted = []
             for k, piece in enumerate(pieces):
-                n0 = sum(pieces[:k])
+                n0 = first + sum(pieces[:k])
                 part = sbuf("parted_%d_%d" % (c, n0), [P, 2, piece], U16)
                 nc.vector.tensor_copy(
                     part[:], both[:, n0 : n0 + piece].bitcast(U16).rearrange("p (n d) -> p d n", d=2)
@@ -108,52 +104,52 @@ def tile_list_kvt_no_exp_kernel(
             return parted
 
         def project(step, copy, dst, w, w_s, w_dtype, rhs, rhs_s):
-            name = "bank%d" % (step % KEY_BANKS)
-            bank = psum.tile([P, 4, NB], F32, name=name, tag=name)
+            name = "bank%d" % step
+            bank = psum.tile([P, 4, NB], F32, name=name, tag=name, offset=(step % KEY_BANKS) * BANK)
             for t in range(4):
-                for a in range(2):
+                for a in (1, 0):
                     nc.tensor.matmul_mx(
                         bank[:, t, :],
                         lhsT=w[:, t, a, :].bitcast(w_dtype),
-                        lhsT_scale=w_s[:, t, a, :].bitcast(U8),
+                        lhsT_scale=w_s[a][:, t * P : (t + 1) * P],
                         rhs=rhs[a],
                         rhs_scale=rhs_s[a],
-                        start=(a == 0),
-                        stop=(a == 1),
+                        start=(a == 1),
+                        stop=(a == 0),
                     )
             copy(dst, bank[:].rearrange("p t n -> p n t"))
 
-        def keys(c, step, parted, planes, base, widths, copies, tag=None):
+        def keys(step, parted, planes, base, widths, copy, first_copy=None):
             units = []
             i = 0
             for u, width in enumerate(widths):
-                kb = sbuf("kb_%d_%d" % (step, u), [P, width, 4], BF16, tag=tag)
+                kb = sbuf("kb_%d_%d" % (step, u), [P, width, 4], BF16)
                 for h in range(width // NB):
                     n0 = base + i * NB
                     project(
-                        step + i, copies[i], kb[:, h * NB : (h + 1) * NB, :], wk, wk_s, FP4X4,
+                        step + i, first_copy if i == 0 and first_copy else copy, kb[:, h * NB : (h + 1) * NB, :], wk, wk_s, FP4X4,
                         [parted[i][:, a, :].bitcast(FP4X4) for a in range(2)],
-                        [planes[:, a, n0 : n0 + NB] for a in range(2)],
+                        [planes[a][:, n0 : n0 + NB] for a in range(2)],
                     )
                     i = i + 1
                 units.append(kb)
             return units
 
-        def quantise(name, src, width, codes=None):
-            if codes is None:
-                codes = sbuf(name + "_codes", [P, width], U32)[:]
+        def quantise(name, src, width):
+            codes = sbuf(name + "_codes", [P, width], U32)
             scales = sbuf(name + "_scales", [P, width], U8)
-            nc.vector.quantize_mx(codes.bitcast(FP8X4), scales[:], src)
+            nc.vector.quantize_mx(codes[:].bitcast(FP8X4), scales[:], src)
             return codes, scales
 
         out_view = out.rearrange("(h p) j -> p h j", h=2)
 
-        def quantise_keys(name, kb, width, codes=None):
-            return quantise(name, kb[:].rearrange("p n t -> p (n t)"), width, codes)
+        def quantise_keys(name, kb, width):
+            return quantise(name, kb[:].rearrange("p n t -> p (n t)"), width)
 
         def scores(u, j0, width, k_codes, k_scales, queue):
-            name = "acc%d" % (u % SCORE_BANKS)
-            acc = psum.tile([P, 2, width], F32, name=name, tag=name)
+            name = "acc%d" % u
+            place = 14 % KEY_BANKS if u == 2 else KEY_BANKS + u % SCORE_BANKS
+            acc = psum.tile([P, 2, width], F32, name=name, tag=name, offset=place * BANK)
             for h in range(2):
                 nc.tensor.matmul_mx(
                     acc[:, h, :],
@@ -168,38 +164,48 @@ def tile_list_kvt_no_exp_kernel(
             nc.scalar.activation(res[:], acc[:], EXP, scale=0.015625)
             queue.dma_start(out_view[:, :, j0 : j0 + width], res[:])
 
-        planes_a = place_scales("planes_a", gather_scales("rows_a", 0, FIRST, "w_raw"), FIRST, "planes_a")
+        def chunk_scores(c, quantised):
+            codes, scales = quantised
+            for u in range(2):
+                cols = slice(u * UNIT, (u + 1) * UNIT)
+                scores(2 * c + u, c * CH + u * UNIT, UNIT, codes[:, cols], scales[:, cols], nc.sync)
 
         warm_in = sbuf("warm_in", [P, 1], F32)
         warm_out = sbuf("warm_out", [P, 1], F32)
-        nc.vector.memset(warm_in[:], 0.0)
+        nc.gpsimd.memset(warm_in[:], 0.0)
         nc.scalar.activation(warm_out[:], warm_in[:], EXP)
 
+        rows_0 = gather_scales("rows_0", 0, CH)
+        joined = sbuf("joined", [P, (CH + 2 * R) // 4], I32)
+        nc.vector.tensor_copy(
+            joined[:, CH // 4 :].rearrange("p (v t b w) -> p v t b w", v=2, t=4, w=2),
+            ws_raw[:].rearrange("p (v b t w) -> p v t b w", v=2, t=4, w=2),
+        )
+        nc.vector.tensor_copy(joined[:, 0 : CH // 4], rows_0[:].bitcast(I32))
+        planes_0 = place_scales("planes_0", joined, CH + 2 * R)
+        wk_s = [plane[:, CH : CH + R] for plane in planes_0]
+        wq_s = [plane[:, CH + R :] for plane in planes_0]
+        planes_12 = place_scales("planes_12", gather_scales("rows_12", CH, 3 * CH)[:].bitcast(I32), 2 * CH)
+        wk = sbuf("wk", [P, 4, 2, 64], I32)
         deal(wk[:], wk_raw[:], 4)
-        deal(wk_s[0:100], wk_s_raw[0:100], 2)
-        rows_b = gather_scales("rows_b", FIRST, J, "wk_raw")
-        warm = psum.tile([P, CH], F32, name="acc2", tag="acc2")
-        wk_flat = wk[:].rearrange("p t a n -> p (t a n)").bitcast(FP4X4)
-        wk_s_flat = wk_s.rearrange("p t a n -> p (t a n)").bitcast(U8)
-        for i in range(4):
-            nc.tensor.matmul_mx(
-                warm[:], lhsT=wk_flat[:, 0:P], lhsT_scale=wk_s_flat[:, 0:P],
-                rhs=wk_flat[:, 0:CH], rhs_scale=wk_s_flat[:, 0:CH], start=True, stop=True,
-            )
-        on_scalar = [nc.scalar.copy] * 4
-        on_vector = [nc.vector.tensor_copy] * 4
-        parted0 = gather_words(0, "both_0", [128, 128, 256])
-        kb0 = keys(0, 0, parted0, planes_a, 0, [CH], on_scalar)
-        parted1 = gather_words(1, "both_1", [CH])
-
         x_raw = sbuf("x_raw", [P, 2, 4, M], F32)
         nc.sync.dma_start(x_raw[:], x.rearrange("(a p i) m -> p a i m", a=2, i=4))
-        for q in range(4):
-            load_scale_rows(wk_s_raw, wq_scales, q, nc.sync)
+
+        warm = psum.tile([P, CH], F32, name="warm", tag="warm", offset=(KEY_BANKS + SCORE_BANKS - 1) * BANK)
+        for i in range(4):
+            nc.tensor.matmul_mx(
+                warm[:], lhsT=tab_w[:, 0 : P // 2].bitcast(FP4X4), lhsT_scale=tab_s[:, 0:P],
+                rhs=tab_w[:, 0 : CH // 2].bitcast(FP4X4), rhs_scale=tab_s[:, 0:CH], start=True, stop=True,
+            )
+
+        both_01 = sbuf("both_01", [P, 2 * CH - NB], U32)
+        kb0 = keys(0, part_words(0, gather_words(0, both_01[:, CH - NB :]), 0, [NB, NB, UNIT]), planes_0, 0, [CH], nc.scalar.copy)
         wq_raw = sbuf("wq_raw", [P, 2, R], I32)
         nc.sync.dma_start(wq_raw[:], wq_words.rearrange("a p r i -> p a (r i)").bitcast(I32))
-        planes_b = place_scales("planes_b", rows_b, J - FIRST, "both_1")
-        kb1 = keys(1, 4, parted1, planes_a, CH, [CH], on_scalar)
+        kb1 = keys(4, part_words(1, gather_words(1, both_01[:, 0:CH]), 0, [CH]), planes_12, 0, [CH], nc.scalar.copy)
+        both_2 = gather_words(2, sbuf("both_2", [P, CH], U32)[:])
+        planes_3 = place_scales("planes_3", gather_scales("rows_3", 3 * CH, J)[:].bitcast(I32), CH)
+        kb2 = keys(8, part_words(2, both_2, 0, [UNIT]), planes_12, CH, [UNIT], nc.scalar.copy)
 
         xb = sbuf("xb", [P, 2, M, 4], BF16)
         nc.vector.tensor_copy(
@@ -207,32 +213,31 @@ def tile_list_kvt_no_exp_kernel(
             x_raw[:].rearrange("p a i (c j) -> p a c i j", j=4),
         )
         x_codes, x_scales = quantise("x", xb[:].rearrange("p a m i -> p (a m i)"), 2 * M)
-        deal(wq_s[0:100], wk_s_raw[0:100], 2)
         wq = sbuf("wq", [P, 4, 2, 128], I32)
         deal(wq[:], wq_raw[:], 8)
         qb = sbuf("qb", [P, M, 4], BF16)
         for h in range(M // NB):
             project(
-                8 + h, nc.scalar.copy, qb[:, h * NB : (h + 1) * NB, :], wq, wq_s, FP8X4,
+                10 + h, nc.scalar.copy, qb[:, h * NB : (h + 1) * NB, :], wq, wq_s, FP8X4,
                 [x_codes[:, a * M + h * NB : a * M + (h + 1) * NB].bitcast(FP8X4) for a in range(2)],
                 [x_scales[:, a * M + h * NB : a * M + (h + 1) * NB] for a in range(2)],
             )
-        parted2 = gather_words(2, "both_2", [UNIT, UNIT])
-        parted3 = gather_words(3, "both_3", [CH])
+        kb2 = kb2 + keys(12, part_words(2, both_2, UNIT, [UNIT]), planes_12, CH + UNIT, [UNIT], nc.scalar.copy)
+        k0 = quantise_keys("k0", kb0[0], CH)
+        both_3 = gather_words(3, sbuf("both_3", [P, CH], U32)[:])
         q_codes, q_scales = quantise("q", qb[:].rearrange("p m t -> p (m t)"), M)
-        early_codes = sbuf("early_codes", [P, 2, CH], U32)
-        early = [quantise_keys("k%d" % c, kb, CH, early_codes[:, c, :]) for c, kb in enumerate(kb0 + kb1)]
-        kb2 = keys(2, 10, parted2, planes_a, 2 * CH, [UNIT, UNIT], on_scalar)
-        mid = [quantise_keys("k%d" % (2 + u), kb, UNIT) for u, kb in enumerate(kb2)]
-        kb3 = keys(3, 14, parted3[:1], planes_b, 0, [NB], on_vector)
-        for u in range(4):
-            codes, scales = early[u // 2]
-            cols = slice((u % 2) * UNIT, (u % 2 + 1) * UNIT)
-            scores(u, u * UNIT, UNIT, codes[:, cols], scales[:, cols], nc.sync)
-        kb3 = kb3 + keys(3, 15, parted3[1:2], planes_b, NB, [NB], on_vector)
-        for u in range(2):
-            scores(4 + u, 2 * CH + u * UNIT, UNIT, mid[u][0], mid[u][1][:], nc.sync)
-        kb3 = kb3 + keys(3, 16, parted3[2:], planes_b, 2 * NB, [NB, NB], on_vector)
+        chunk_scores(0, k0)
+        parted3 = part_words(3, both_3, 0, [NB, 3 * NB])
+        k1 = quantise_keys("k1", kb1[0], CH)
+        k2 = [quantise_keys("k2_%d" % u, kb, UNIT) for u, kb in enumerate(kb2)]
+        kb3 = keys(14, parted3[:2], planes_3, 0, [UNIT], nc.vector.tensor_copy, nc.scalar.copy)
+        chunk_scores(1, k1)
+        kb3 = kb3 + keys(16, parted3[2:], planes_3, 2 * NB, [NB, NB], nc.vector.tensor_copy)
+        for u, (codes, scales) in enumerate(k2):
+            scores(4 + u, 2 * CH + u * UNIT, UNIT, codes[:], scales[:], nc.sync)
+        j0 = 3 * CH
         for u, kb in enumerate(kb3):
-            codes, scales = quantise_keys("k%d" % (4 + u), kb, NB)
-            scores(6 + u, 3 * CH + u * NB, NB, codes, scales[:], nc.scalar if u == 3 else nc.sync)
+            width = kb.shape[1]
+            codes, scales = quantise_keys("k%d" % (3 + u), kb, width)
+            scores(6 + u, j0, width, codes[:], scales[:], nc.scalar if u == 2 else nc.sync)
+            j0 = j0 + width

@@ -22,11 +22,12 @@ UNIT = 256
 KEY_BANKS = 5
 SCORE_BANKS = 3
 PLACES = {
-    "rows_0": 0, "rows_12": 0, "joined": 1024, "x_raw": 1024,
-    "wk_raw": 9216, "parted_0_128": 9216, "parted_0_256": 9728, "parted_0_0": 10752, "wq_raw": 10752,
-    "both_01": 14848, "both_2": 14848, "rows_3": 16896, "k0_codes": 13312, "both_3": 15360,
-    "qb": 17408, "k1_codes": 16384, "parted_3_0": 18432, "k2_0_codes": 18944,
-    "xb": 20480, "parted_2_256": 20480,
+    "wks_raw": 0, "x_raw": 0,
+    "wq_raw": 8192, "rows_01": 11776, "wqs_raw": 12288,
+    "k0_codes": 8192, "both_3": 10752, "parted_2_256": 12800,
+    "both_012": 14336,
+    "wk_raw": 20480, "parted_0_128": 20480, "parted_0_0": 22016,
+    "qb": 24576, "k1_codes": 23040, "parted_3_0": 25088, "k2_codes": 25600,
 }
 BANK = 2048
 
@@ -45,29 +46,34 @@ def tile_list_kvt_no_exp_kernel(
                 return reuse.tile(shape, dtype, name=name, tag=name, align_bytes=64, offset=PLACES[name])
             return held.tile(shape, dtype, name=name, tag=name, align_bytes=64)
 
-        def load_scale_rows(dst, dram):
-            rows = dram.rearrange("a (h u r) t -> u (a h) r t", h=2, u=2).bitcast(I32)
-            for u in range(2):
-                nc.sync.dma_start(dst[48 + 32 * u : 64 + 32 * u], rows[u])
-
-        def clear_other_rows(engine, tile_words):
-            for lo, hi in [(0, 48), (64, 80), (96, P)]:
-                engine.memset(tile_words[lo:hi], 0)
-
         offsets = held.tile([P, J // 16], U16, name="offsets")
         nc.sync.dma_start(offsets[:], offs)
         tab_s = sbuf("tab_s", [P, T], U8)
-        load_scale_rows(tab_s[:].bitcast(I32), tab_scales)
-        ws_raw = sbuf("ws_raw", [P, 2 * R // 4], I32)
-        load_scale_rows(ws_raw[:, 0 : R // 4], wk_scales)
-        load_scale_rows(ws_raw[:, R // 4 :], wq_scales)
+        table_rows = tab_scales.rearrange("a (h u r) t -> u (a h) r t", h=2, u=2).bitcast(I32)
+        for u in range(2):
+            nc.sync.dma_start(tab_s[48 + 32 * u : 64 + 32 * u, :].bitcast(I32), table_rows[u])
+
+        wks_raw = sbuf("wks_raw", [P, 2, R // 4], I32)
+
+        def load_scale_rows(raw, dram, q, queue):
+            queue.dma_start(
+                raw[32 * q : 32 * q + 4, :, :],
+                dram[:, 4 * q : 4 * q + 4, :].rearrange("a r n -> r a n").bitcast(I32),
+            )
+
+        load_scale_rows(wks_raw, wk_scales, 3, nc.sync)
         tab_w = sbuf("tab_w", [P, T], I32)
         nc.sync.dma_start(tab_w[:], tab_words[0].rearrange("p t b -> p (t b)").bitcast(I32))
         wk_raw = sbuf("wk_raw", [P, 2, R // 2], I32)
         nc.sync.dma_start(wk_raw[:], wk_words.rearrange("a p n -> p a n").bitcast(I32))
+
+        nc.gpsimd.memset(wks_raw[0:96], 0)
+        for q in range(3):
+            load_scale_rows(wks_raw, wk_scales, q, nc.scalar)
         for engine, lo, hi in [(nc.vector, 0, 48), (nc.vector, 64, 80), (nc.gpsimd, 96, P)]:
             engine.memset(tab_s[lo:hi, :].bitcast(I32), 0)
-        clear_other_rows(nc.gpsimd, ws_raw[:])
+        w_scales = sbuf("w_scales", [P, 2, 4, 2, 32], I32)
+        nc.gpsimd.memset(w_scales[96:P], 0)
 
         def deal(dealt, raw, run):
             nc.vector.tensor_copy(
@@ -89,7 +95,8 @@ def tile_list_kvt_no_exp_kernel(
             return planes
 
         def gather_words(c, both):
-            nc.vector.tensor_copy(both, tab_w[:].bitcast(U32).indirect(offsets[:, 32 * c : 32 * (c + 1)]))
+            columns = slice(c * CH // 16, (c * CH + both.shape[1]) // 16)
+            nc.vector.tensor_copy(both, tab_w[:].bitcast(U32).indirect(offsets[:, columns]))
             return both
 
         def part_words(c, both, first, pieces):
@@ -111,7 +118,7 @@ def tile_list_kvt_no_exp_kernel(
                     nc.tensor.matmul_mx(
                         bank[:, t, :],
                         lhsT=w[:, t, a, :].bitcast(w_dtype),
-                        lhsT_scale=w_s[a][:, t * P : (t + 1) * P],
+                        lhsT_scale=w_s[:, t, a, :].bitcast(U8),
                         rhs=rhs[a],
                         rhs_scale=rhs_s[a],
                         start=(a == 1),
@@ -119,21 +126,19 @@ def tile_list_kvt_no_exp_kernel(
                     )
             copy(dst, bank[:].rearrange("p t n -> p n t"))
 
-        def keys(step, parted, planes, base, widths, copy, first_copy=None):
-            units = []
-            i = 0
-            for u, width in enumerate(widths):
-                kb = sbuf("kb_%d_%d" % (step, u), [P, width, 4], BF16)
-                for h in range(width // NB):
-                    n0 = base + i * NB
-                    project(
-                        step + i, first_copy if i == 0 and first_copy else copy, kb[:, h * NB : (h + 1) * NB, :], wk, wk_s, FP4X4,
-                        [parted[i][:, a, :].bitcast(FP4X4) for a in range(2)],
-                        [planes[a][:, n0 : n0 + NB] for a in range(2)],
-                    )
-                    i = i + 1
-                units.append(kb)
-            return units
+        def keys_into(kb, step, parted, planes, base, copy):
+            for i, part in enumerate(parted):
+                n0 = base + i * NB
+                project(
+                    step + i, copy, kb[:, i * NB : (i + 1) * NB, :], wk, wk_s, FP4X4,
+                    [part[:, a, :].bitcast(FP4X4) for a in range(2)],
+                    [planes[a][:, n0 : n0 + NB] for a in range(2)],
+                )
+
+        def keys(step, parted, planes, base, copy):
+            kb = sbuf("kb_%d" % step, [P, len(parted) * NB, 4], BF16)
+            keys_into(kb[:], step, parted, planes, base, copy)
+            return kb
 
         def quantise(name, src, width):
             codes = sbuf(name + "_codes", [P, width], U32)
@@ -146,50 +151,55 @@ def tile_list_kvt_no_exp_kernel(
         def quantise_keys(name, kb, width):
             return quantise(name, kb[:].rearrange("p n t -> p (n t)"), width)
 
-        def scores(u, j0, width, k_codes, k_scales, queue):
+        def score_pass(acc, h, k_codes, k_scales):
+            nc.tensor.matmul_mx(
+                acc,
+                lhsT=q_codes[:, h * P : (h + 1) * P].bitcast(FP8X4),
+                lhsT_scale=q_scales[:, h * P : (h + 1) * P],
+                rhs=k_codes.bitcast(FP8X4),
+                rhs_scale=k_scales,
+                start=True,
+                stop=True,
+            )
+
+        def score_bank(u, shape):
             name = "acc%d" % u
-            place = 14 % KEY_BANKS if u == 2 else KEY_BANKS + u % SCORE_BANKS
-            acc = psum.tile([P, 2, width], F32, name=name, tag=name, offset=place * BANK)
+            return psum.tile(shape, F32, name=name, tag=name, offset=(KEY_BANKS + u % SCORE_BANKS) * BANK)
+
+        def scores(u, j0, width, k_codes, k_scales, queue):
+            acc = score_bank(u, [P, 2, width])
             for h in range(2):
-                nc.tensor.matmul_mx(
-                    acc[:, h, :],
-                    lhsT=q_codes[:, h * P : (h + 1) * P].bitcast(FP8X4),
-                    lhsT_scale=q_scales[:, h * P : (h + 1) * P],
-                    rhs=k_codes.bitcast(FP8X4),
-                    rhs_scale=k_scales,
-                    start=True,
-                    stop=True,
-                )
+                score_pass(acc[:, h, :], h, k_codes, k_scales)
             res = sbuf("res_%d" % u, [P, 2, width], F32)
             nc.scalar.activation(res[:], acc[:], EXP, scale=0.015625)
             queue.dma_start(out_view[:, :, j0 : j0 + width], res[:])
 
         def chunk_scores(c, quantised):
             codes, scales = quantised
-            for u in range(2):
-                cols = slice(u * UNIT, (u + 1) * UNIT)
-                scores(2 * c + u, c * CH + u * UNIT, UNIT, codes[:, cols], scales[:, cols], nc.sync)
+            for h in range(2):
+                acc = score_bank(2 * c + h, [P, CH])
+                score_pass(acc[:], h, codes[:], scales[:])
+                res = sbuf("res_%d" % (2 * c + h), [P, CH], F32)
+                nc.scalar.activation(res[:], acc[:], EXP, scale=0.015625)
+                nc.sync.dma_start(out_view[:, h, c * CH : (c + 1) * CH], res[:])
 
         warm_in = sbuf("warm_in", [P, 1], F32)
         warm_out = sbuf("warm_out", [P, 1], F32)
         nc.gpsimd.memset(warm_in[:], 0.0)
         nc.scalar.activation(warm_out[:], warm_in[:], EXP)
 
-        rows_0 = gather_scales("rows_0", 0, CH)
-        joined = sbuf("joined", [P, (CH + 2 * R) // 4], I32)
-        nc.vector.tensor_copy(
-            joined[:, CH // 4 :].rearrange("p (v t b w) -> p v t b w", v=2, t=4, w=2),
-            ws_raw[:].rearrange("p (v b t w) -> p v t b w", v=2, t=4, w=2),
-        )
-        nc.vector.tensor_copy(joined[:, 0 : CH // 4], rows_0[:].bitcast(I32))
-        planes_0 = place_scales("planes_0", joined, CH + 2 * R)
-        wk_s = [plane[:, CH : CH + R] for plane in planes_0]
-        wq_s = [plane[:, CH + R :] for plane in planes_0]
-        planes_12 = place_scales("planes_12", gather_scales("rows_12", CH, 3 * CH)[:].bitcast(I32), 2 * CH)
-        wk = sbuf("wk", [P, 4, 2, 64], I32)
-        deal(wk[:], wk_raw[:], 4)
+        planes_01 = place_scales("planes_01", gather_scales("rows_01", 0, 2 * CH)[:].bitcast(I32), 2 * CH)
+        wk_s, wq_s = w_scales[:, 0], w_scales[:, 1]
+        deal(wk_s[0:100], wks_raw[0:100], 2)
         x_raw = sbuf("x_raw", [P, 2, 4, M], F32)
         nc.sync.dma_start(x_raw[:], x.rearrange("(a p i) m -> p a i m", a=2, i=4))
+        planes_23 = place_scales("planes_23", gather_scales("rows_23", 2 * CH, J)[:].bitcast(I32), 2 * CH)
+        wq_raw = sbuf("wq_raw", [P, 2, R], I32)
+        nc.sync.dma_start(wq_raw[:], wq_words.rearrange("a p r i -> p a (r i)").bitcast(I32))
+        wqs_raw = sbuf("wqs_raw", [P, 2, R // 4], I32)
+        nc.gpsimd.memset(wqs_raw[:], 0)
+        for q in range(4):
+            load_scale_rows(wqs_raw, wq_scales, q, nc.sync)
 
         warm = psum.tile([P, CH], F32, name="warm", tag="warm", offset=(KEY_BANKS + SCORE_BANKS - 1) * BANK)
         for i in range(4):
@@ -198,23 +208,28 @@ def tile_list_kvt_no_exp_kernel(
                 rhs=tab_w[:, 0 : CH // 2].bitcast(FP4X4), rhs_scale=tab_s[:, 0:CH], start=True, stop=True,
             )
 
-        both_01 = sbuf("both_01", [P, 2 * CH - NB], U32)
-        kb0 = keys(0, part_words(0, gather_words(0, both_01[:, CH - NB :]), 0, [NB, NB, UNIT]), planes_0, 0, [CH], nc.scalar.copy)
-        wq_raw = sbuf("wq_raw", [P, 2, R], I32)
-        nc.sync.dma_start(wq_raw[:], wq_words.rearrange("a p r i -> p a (r i)").bitcast(I32))
-        kb1 = keys(4, part_words(1, gather_words(1, both_01[:, 0:CH]), 0, [CH]), planes_12, 0, [CH], nc.scalar.copy)
-        both_2 = gather_words(2, sbuf("both_2", [P, CH], U32)[:])
-        planes_3 = place_scales("planes_3", gather_scales("rows_3", 3 * CH, J)[:].bitcast(I32), CH)
-        kb2 = keys(8, part_words(2, both_2, 0, [UNIT]), planes_12, CH, [UNIT], nc.scalar.copy)
+        both_012 = sbuf("both_012", [P, 3 * CH - NB], U32)
+        both_0 = gather_words(0, both_012[:, 2 * CH - NB :])
+        wk = sbuf("wk", [P, 4, 2, 64], I32)
+        deal(wk[:], wk_raw[:], 4)
+        parted0 = part_words(0, both_0, 0, [NB, 3 * NB])
+        kb0 = keys(0, parted0, planes_01, 0, nc.scalar.copy)
+        both_12 = gather_words(1, both_012[:, 0 : 2 * CH])
+        parted1 = part_words(1, both_12[:, 0:CH], 0, [CH])
+        kb1 = keys(4, parted1, planes_01, CH, nc.scalar.copy)
 
+        parted2 = part_words(2, both_12[:, CH:], 0, [UNIT])
+        kb2 = sbuf("kb2", [P, CH, 4], BF16)
+        keys_into(kb2[:, 0:UNIT], 8, parted2, planes_23, 0, nc.scalar.copy)
         xb = sbuf("xb", [P, 2, M, 4], BF16)
         nc.vector.tensor_copy(
             xb[:].rearrange("p a (c j) i -> p a c i j", j=4),
             x_raw[:].rearrange("p a i (c j) -> p a c i j", j=4),
         )
-        x_codes, x_scales = quantise("x", xb[:].rearrange("p a m i -> p (a m i)"), 2 * M)
         wq = sbuf("wq", [P, 4, 2, 128], I32)
         deal(wq[:], wq_raw[:], 8)
+        x_codes, x_scales = quantise("x", xb[:].rearrange("p a m i -> p (a m i)"), 2 * M)
+        deal(wq_s[0:100], wqs_raw[0:100], 2)
         qb = sbuf("qb", [P, M, 4], BF16)
         for h in range(M // NB):
             project(
@@ -222,19 +237,22 @@ def tile_list_kvt_no_exp_kernel(
                 [x_codes[:, a * M + h * NB : a * M + (h + 1) * NB].bitcast(FP8X4) for a in range(2)],
                 [x_scales[:, a * M + h * NB : a * M + (h + 1) * NB] for a in range(2)],
             )
-        kb2 = kb2 + keys(12, part_words(2, both_2, UNIT, [UNIT]), planes_12, CH + UNIT, [UNIT], nc.scalar.copy)
-        k0 = quantise_keys("k0", kb0[0], CH)
+        parted2 = part_words(2, both_12[:, CH:], UNIT, [UNIT])
+        keys_into(kb2[:, UNIT:], 12, parted2, planes_23, UNIT, nc.scalar.copy)
         both_3 = gather_words(3, sbuf("both_3", [P, CH], U32)[:])
+        k0 = quantise_keys("k0", kb0, CH)
         q_codes, q_scales = quantise("q", qb[:].rearrange("p m t -> p (m t)"), M)
         chunk_scores(0, k0)
         parted3 = part_words(3, both_3, 0, [NB, 3 * NB])
-        k1 = quantise_keys("k1", kb1[0], CH)
-        k2 = [quantise_keys("k2_%d" % u, kb, UNIT) for u, kb in enumerate(kb2)]
-        kb3 = keys(14, parted3[:2], planes_3, 0, [UNIT], nc.vector.tensor_copy, nc.scalar.copy)
+        k1 = quantise_keys("k1", kb1, CH)
+        k2 = quantise_keys("k2", kb2, CH)
+        kb3 = [sbuf("kb_14", [P, UNIT, 4], BF16)]
+        keys_into(kb3[0][:, 0:NB], 14, parted3[:1], planes_23, CH, nc.scalar.copy)
         chunk_scores(1, k1)
-        kb3 = kb3 + keys(16, parted3[2:], planes_3, 2 * NB, [NB, NB], nc.vector.tensor_copy)
-        for u, (codes, scales) in enumerate(k2):
-            scores(4 + u, 2 * CH + u * UNIT, UNIT, codes[:], scales[:], nc.sync)
+        keys_into(kb3[0][:, NB:], 15, parted3[1:2], planes_23, CH + NB, nc.vector.tensor_copy)
+        kb3.append(keys(16, parted3[2:3], planes_23, CH + 2 * NB, nc.vector.tensor_copy))
+        chunk_scores(2, k2)
+        kb3.append(keys(17, parted3[3:], planes_23, CH + 3 * NB, nc.vector.tensor_copy))
         j0 = 3 * CH
         for u, kb in enumerate(kb3):
             width = kb.shape[1]

@@ -24,7 +24,7 @@ SCORE_BANKS = 3
 PLACES = {
     "wks_raw": 0, "x_raw": 0,
     "wq_raw": 8192, "rows_01": 11776, "wqs_raw": 12288,
-    "k0_codes": 8192, "both_3": 10752, "parted_2_256": 12800,
+    "k0_codes": 8192, "both_3": 10752, "parted_2_384": 12800,
     "both_012": 14336,
     "wk_raw": 20480, "parted_0_128": 20480, "parted_0_0": 22016,
     "qb": 24576, "k1_codes": 23040, "parted_3_0": 25088, "k2_codes": 25600,
@@ -218,14 +218,15 @@ def tile_list_kvt_no_exp_kernel(
         parted1 = part_words(1, both_12[:, 0:CH], 0, [CH])
         kb1 = keys(4, parted1, planes_01, CH, nc.scalar.copy)
 
-        parted2 = part_words(2, both_12[:, CH:], 0, [UNIT])
+        parted2 = part_words(2, both_12[:, CH:], 0, [3 * NB])
         kb2 = sbuf("kb2", [P, CH, 4], BF16)
-        keys_into(kb2[:, 0:UNIT], 8, parted2, planes_23, 0, nc.scalar.copy)
+        keys_into(kb2[:, 0 : 3 * NB], 8, parted2, planes_23, 0, nc.scalar.copy)
         xb = sbuf("xb", [P, 2, M, 4], BF16)
-        nc.vector.tensor_copy(
-            xb[:].rearrange("p a (c j) i -> p a c i j", j=4),
-            x_raw[:].rearrange("p a i (c j) -> p a c i j", j=4),
-        )
+        for a, copy in enumerate([nc.scalar.copy, nc.vector.tensor_copy]):
+            copy(
+                xb[:, a].rearrange("p (c j) i -> p c i j", j=4),
+                x_raw[:, a].rearrange("p i (c j) -> p c i j", j=4),
+            )
         wq = sbuf("wq", [P, 4, 2, 128], I32)
         deal(wq[:], wq_raw[:], 8)
         x_codes, x_scales = quantise("x", xb[:].rearrange("p a m i -> p (a m i)"), 2 * M)
@@ -233,12 +234,12 @@ def tile_list_kvt_no_exp_kernel(
         qb = sbuf("qb", [P, M, 4], BF16)
         for h in range(M // NB):
             project(
-                10 + h, nc.scalar.copy, qb[:, h * NB : (h + 1) * NB, :], wq, wq_s, FP8X4,
+                11 + h, nc.scalar.copy, qb[:, h * NB : (h + 1) * NB, :], wq, wq_s, FP8X4,
                 [x_codes[:, a * M + h * NB : a * M + (h + 1) * NB].bitcast(FP8X4) for a in range(2)],
                 [x_scales[:, a * M + h * NB : a * M + (h + 1) * NB] for a in range(2)],
             )
-        parted2 = part_words(2, both_12[:, CH:], UNIT, [UNIT])
-        keys_into(kb2[:, UNIT:], 12, parted2, planes_23, UNIT, nc.scalar.copy)
+        parted2 = part_words(2, both_12[:, CH:], 3 * NB, [NB])
+        keys_into(kb2[:, 3 * NB :], 13, parted2, planes_23, 3 * NB, nc.scalar.copy)
         both_3 = gather_words(3, sbuf("both_3", [P, CH], U32)[:])
         k0 = quantise_keys("k0", kb0, CH)
         q_codes, q_scales = quantise("q", qb[:].rearrange("p m t -> p (m t)"), M)
@@ -247,7 +248,7 @@ def tile_list_kvt_no_exp_kernel(
         k1 = quantise_keys("k1", kb1, CH)
         k2 = quantise_keys("k2", kb2, CH)
         kb3 = [sbuf("kb_14", [P, UNIT, 4], BF16)]
-        keys_into(kb3[0][:, 0:NB], 14, parted3[:1], planes_23, CH, nc.scalar.copy)
+        keys_into(kb3[0][:, 0:NB], 14, parted3[:1], planes_23, CH, nc.vector.tensor_copy)
         chunk_scores(1, k1)
         keys_into(kb3[0][:, NB:], 15, parted3[1:2], planes_23, CH + NB, nc.vector.tensor_copy)
         kb3.append(keys(16, parted3[2:3], planes_23, CH + 2 * NB, nc.vector.tensor_copy))

@@ -26,7 +26,7 @@ PLACES = {
     "wq_raw": 8192, "rows_01": 11776, "wqs_raw": 12288,
     "k0_codes": 8192, "both_3": 10752, "parted_2_384": 12800,
     "both_012": 14336,
-    "wk_raw": 20480, "parted_0_128": 20480, "parted_0_0": 22016,
+
     "qb": 24576, "k1_codes": 23040, "parted_3_0": 25088, "k2_codes": 25600,
 }
 BANK = 2048
@@ -75,8 +75,8 @@ def tile_list_kvt_no_exp_kernel(
         w_scales = sbuf("w_scales", [P, 2, 4, 2, 32], I32)
         nc.gpsimd.memset(w_scales[96:P], 0)
 
-        def deal(dealt, raw, run):
-            nc.vector.tensor_copy(
+        def deal(engine, dealt, raw, run):
+            engine.tensor_copy(
                 dealt.rearrange("p t a (b w) -> p t (a b) w", w=run),
                 raw.rearrange("p a (b t w) -> p t (a b) w", t=4, w=run),
             )
@@ -190,7 +190,7 @@ def tile_list_kvt_no_exp_kernel(
 
         planes_01 = place_scales("planes_01", gather_scales("rows_01", 0, 2 * CH)[:].bitcast(I32), 2 * CH)
         wk_s, wq_s = w_scales[:, 0], w_scales[:, 1]
-        deal(wk_s[0:100], wks_raw[0:100], 2)
+        deal(nc.gpsimd, wk_s[0:100], wks_raw[0:100], 2)
         x_raw = sbuf("x_raw", [P, 2, 4, M], F32)
         nc.sync.dma_start(x_raw[:], x.rearrange("(a p i) m -> p a i m", a=2, i=4))
         planes_23 = place_scales("planes_23", gather_scales("rows_23", 2 * CH, J)[:].bitcast(I32), 2 * CH)
@@ -211,7 +211,7 @@ def tile_list_kvt_no_exp_kernel(
         both_012 = sbuf("both_012", [P, 3 * CH - NB], U32)
         both_0 = gather_words(0, both_012[:, 2 * CH - NB :])
         wk = sbuf("wk", [P, 4, 2, 64], I32)
-        deal(wk[:], wk_raw[:], 4)
+        deal(nc.gpsimd, wk[:], wk_raw[:], 4)
         parted0 = part_words(0, both_0, 0, [NB, 3 * NB])
         kb0 = keys(0, parted0, planes_01, 0, nc.scalar.copy)
         both_12 = gather_words(1, both_012[:, 0 : 2 * CH])
@@ -228,9 +228,9 @@ def tile_list_kvt_no_exp_kernel(
                 x_raw[:, a].rearrange("p i (c j) -> p c i j", j=4),
             )
         wq = sbuf("wq", [P, 4, 2, 128], I32)
-        deal(wq[:], wq_raw[:], 8)
+        deal(nc.gpsimd, wq[:], wq_raw[:], 8)
         x_codes, x_scales = quantise("x", xb[:].rearrange("p a m i -> p (a m i)"), 2 * M)
-        deal(wq_s[0:100], wqs_raw[0:100], 2)
+        deal(nc.gpsimd, wq_s[0:100], wqs_raw[0:100], 2)
         qb = sbuf("qb", [P, M, 4], BF16)
         for h in range(M // NB):
             project(

@@ -19,15 +19,13 @@ P = 128
 CH = 512
 NB = 128
 UNIT = 256
-KEY_BANKS = 5
-SCORE_BANKS = 3
+BANKS = 8
 PLACES = {
-    "wks_raw": 0, "x_raw": 0,
-    "wq_raw": 8192, "rows_01": 11776, "wqs_raw": 12288,
-    "k0_codes": 8192, "both_3": 10752, "parted_2_384": 12800,
-    "both_012": 14336,
-
-    "qb": 24576, "k1_codes": 23040, "parted_3_0": 25088, "k2_codes": 25600,
+    "x0_raw": 0, "wks_raw0": 4032, "wqs_raw": 4096, "x1_raw": 6016,
+    "wq_raw": 10112, "both_2": 10112, "k0_codes": 12160, "wks_raw1": 14144, "rows_1": 14208,
+    "wk_raw": 16384, "both_1": 16384,
+    "qb": 20480, "k1_codes": 18496, "parted_10": 20544, "both_3": 22464,
+    "x_codes": 24576, "kb1_late": 26560,
 }
 BANK = 2048
 
@@ -46,99 +44,97 @@ def tile_list_kvt_no_exp_kernel(
                 return reuse.tile(shape, dtype, name=name, tag=name, align_bytes=64, offset=PLACES[name])
             return held.tile(shape, dtype, name=name, tag=name, align_bytes=64)
 
+        def load_scale_rows(raw, dram, q):
+            nc.sync.dma_start(raw, dram[:, 4 * q : 4 * q + 4, :].rearrange("a r n -> r a n").bitcast(I32))
+
         offsets = held.tile([P, J // 16], U16, name="offsets")
         nc.sync.dma_start(offsets[:], offs)
         tab_s = sbuf("tab_s", [P, T], U8)
-        table_rows = tab_scales.rearrange("a (h u r) t -> u (a h) r t", h=2, u=2).bitcast(I32)
-        for u in range(2):
-            nc.sync.dma_start(tab_s[48 + 32 * u : 64 + 32 * u, :].bitcast(I32), table_rows[u])
-
-        wks_raw = sbuf("wks_raw", [P, 2, R // 4], I32)
-
-        def load_scale_rows(raw, dram, q, queue):
-            queue.dma_start(
-                raw[32 * q : 32 * q + 4, :, :],
-                dram[:, 4 * q : 4 * q + 4, :].rearrange("a r n -> r a n").bitcast(I32),
-            )
-
-        load_scale_rows(wks_raw, wk_scales, 3, nc.sync)
+        nc.sync.dma_start(tab_s[96:P, :].bitcast(I32), tab_scales.rearrange("a s t -> s a t").bitcast(I32))
+        wks_tiles = [sbuf("wks_raw%d" % u, [P, 2, 2, R // 4], I32) for u in range(2)]
+        wks_raw = [wks_tiles[q // 2][32 * q : 32 * q + 4, q % 2] for q in range(4)]
+        for q in range(4):
+            load_scale_rows(wks_raw[q], wk_scales, q)
         tab_w = sbuf("tab_w", [P, T], I32)
         nc.sync.dma_start(tab_w[:], tab_words[0].rearrange("p t b -> p (t b)").bitcast(I32))
         wk_raw = sbuf("wk_raw", [P, 2, R // 2], I32)
         nc.sync.dma_start(wk_raw[:], wk_words.rearrange("a p n -> p a n").bitcast(I32))
 
-        nc.gpsimd.memset(wks_raw[0:96], 0)
-        for q in range(3):
-            load_scale_rows(wks_raw, wk_scales, q, nc.scalar)
-        for engine, lo, hi in [(nc.vector, 0, 48), (nc.vector, 64, 80), (nc.gpsimd, 96, P)]:
-            engine.memset(tab_s[lo:hi, :].bitcast(I32), 0)
-        w_scales = sbuf("w_scales", [P, 2, 4, 2, 32], I32)
-        nc.gpsimd.memset(w_scales[96:P], 0)
+        def cleared_planes(g):
+            planes = sbuf("planes_%d" % g, [P, 2, 2 * CH], U8)
+            nc.gpsimd.memset(planes[:].rearrange("p a n -> p (a n)").bitcast(I32), 0)
+            return planes
 
-        def deal(engine, dealt, raw, run):
-            engine.tensor_copy(
+        nc.vector.memset(tab_s[0:96, :].bitcast(I32), 0)
+        w_scales = sbuf("w_scales", [P, 2, 4, 2, 32], I32)
+        nc.gpsimd.memset(w_scales[:], 0)
+        plane_tiles = [cleared_planes(g) for g in range(2)]
+
+        def deal(copy, dealt, raw, run):
+            copy(
                 dealt.rearrange("p t a (b w) -> p t (a b) w", w=run),
                 raw.rearrange("p a (b t w) -> p t (a b) w", t=4, w=run),
             )
 
-        def gather_scales(name, j0, j1):
-            rows = sbuf(name, [P, j1 - j0], U8)
-            nc.vector.tensor_copy(rows[:], tab_s[:].indirect(offsets[:, j0 // 16 : j1 // 16]))
-            return rows
+        def gather_scales(rows, j0):
+            nc.vector.tensor_copy(rows, tab_s[:].indirect(offsets[:, j0 // 16 : (j0 + rows.shape[1]) // 16]))
 
-        def place_scales(name, row_words, width):
-            planes = [sbuf("%s_%d" % (name, a), [P, width], U8) for a in range(2)]
-            for a in range(2):
-                for h in range(2):
-                    src = 48 + 8 * a + 4 * h
-                    nc.sync.dma_start(planes[a][64 * h : 64 * h + 64, :].bitcast(I32), row_words[src : src + 64, :])
-            return planes
-
-        def gather_words(c, both):
-            columns = slice(c * CH // 16, (c * CH + both.shape[1]) // 16)
-            nc.vector.tensor_copy(both, tab_w[:].bitcast(U32).indirect(offsets[:, columns]))
-            return both
-
-        def part_words(c, both, first, pieces):
-            parted = []
-            for k, piece in enumerate(pieces):
-                n0 = first + sum(pieces[:k])
-                part = sbuf("parted_%d_%d" % (c, n0), [P, 2, piece], U16)
-                nc.vector.tensor_copy(
-                    part[:], both[:, n0 : n0 + piece].bitcast(U16).rearrange("p (n d) -> p d n", d=2)
+        def place_scales(planes, rows):
+            for q in range(4):
+                nc.sync.dma_start(
+                    planes[32 * q : 32 * q + 4].bitcast(I32), rows[96 + 8 * q : 104 + 8 * q, :].bitcast(I32)
                 )
-                parted.extend(part[:, :, n : n + NB] for n in range(0, piece, NB))
-            return parted
+            return [planes[:, a, :] for a in range(2)]
 
-        def project(step, copy, dst, w, w_s, w_dtype, rhs, rhs_s):
+        def gather_words(j0, both):
+            columns = slice(j0 // 16, (j0 + both.shape[1]) // 16)
+            nc.vector.tensor_copy(both, tab_w[:].bitcast(U32).indirect(offsets[:, columns]))
+
+        parted = []
+
+        def part_words(both):
+            piece = both.shape[1]
+            part = sbuf("parted_%d" % len(parted), [P, 2, piece], U16)
+            nc.vector.tensor_copy(part[:], both.bitcast(U16).rearrange("p (n d) -> p d n", d=2))
+            parted.extend(part[:, :, n : n + NB] for n in range(0, piece, NB))
+
+        steps = []
+
+        def next_bank(shape):
+            step = len(steps)
+            steps.append(step)
             name = "bank%d" % step
-            bank = psum.tile([P, 4, NB], F32, name=name, tag=name, offset=(step % KEY_BANKS) * BANK)
+            return psum.tile(shape, F32, name=name, tag=name, offset=(step % BANKS) * BANK)
+
+        def project(w, w_s, w_dtype, rhs, rhs_s):
+            bank = next_bank([P, 4, NB])
             for t in range(4):
-                for a in (1, 0):
+                for a in range(2):
                     nc.tensor.matmul_mx(
                         bank[:, t, :],
                         lhsT=w[:, t, a, :].bitcast(w_dtype),
                         lhsT_scale=w_s[:, t, a, :].bitcast(U8),
                         rhs=rhs[a],
                         rhs_scale=rhs_s[a],
-                        start=(a == 1),
-                        stop=(a == 0),
+                        start=(a == 0),
+                        stop=(a == 1),
                     )
-            copy(dst, bank[:].rearrange("p t n -> p n t"))
+            return bank[:].rearrange("p t n -> p n t")
 
-        def keys_into(kb, step, parted, planes, base, copy):
-            for i, part in enumerate(parted):
-                n0 = base + i * NB
-                project(
-                    step + i, copy, kb[:, i * NB : (i + 1) * NB, :], wk, wk_s, FP4X4,
-                    [part[:, a, :].bitcast(FP4X4) for a in range(2)],
-                    [planes[a][:, n0 : n0 + NB] for a in range(2)],
-                )
+        def key_bank(b):
+            n0 = (b % 8) * NB
+            return project(
+                wk, wk_s, FP4X4,
+                [parted[b][:, a, :].bitcast(FP4X4) for a in range(2)],
+                [planes[b // 8][a][:, n0 : n0 + NB] for a in range(2)],
+            )
 
-        def keys(step, parted, planes, base, copy):
-            kb = sbuf("kb_%d" % step, [P, len(parted) * NB, 4], BF16)
-            keys_into(kb[:], step, parted, planes, base, copy)
-            return kb
+        def key_columns(b):
+            return kb[b // 4][:, (b % 4) * NB : (b % 4 + 1) * NB, :]
+
+        def keys(banks, copy):
+            for b in banks:
+                copy(key_columns(b), key_bank(b))
 
         def quantise(name, src, width):
             codes = sbuf(name + "_codes", [P, width], U32)
@@ -148,8 +144,8 @@ def tile_list_kvt_no_exp_kernel(
 
         out_view = out.rearrange("(h p) j -> p h j", h=2)
 
-        def quantise_keys(name, kb, width):
-            return quantise(name, kb[:].rearrange("p n t -> p (n t)"), width)
+        def quantise_keys(name, src):
+            return quantise(name, src[:].rearrange("p n t -> p (n t)"), src.shape[1])
 
         def score_pass(acc, h, k_codes, k_scales):
             nc.tensor.matmul_mx(
@@ -162,12 +158,8 @@ def tile_list_kvt_no_exp_kernel(
                 stop=True,
             )
 
-        def score_bank(u, shape):
-            name = "acc%d" % u
-            return psum.tile(shape, F32, name=name, tag=name, offset=(KEY_BANKS + u % SCORE_BANKS) * BANK)
-
         def scores(u, j0, width, k_codes, k_scales, queue):
-            acc = score_bank(u, [P, 2, width])
+            acc = next_bank([P, 2, width])
             for h in range(2):
                 score_pass(acc[:, h, :], h, k_codes, k_scales)
             res = sbuf("res_%d" % u, [P, 2, width], F32)
@@ -177,7 +169,7 @@ def tile_list_kvt_no_exp_kernel(
         def chunk_scores(c, quantised):
             codes, scales = quantised
             for h in range(2):
-                acc = score_bank(2 * c + h, [P, CH])
+                acc = next_bank([P, CH])
                 score_pass(acc[:], h, codes[:], scales[:])
                 res = sbuf("res_%d" % (2 * c + h), [P, CH], F32)
                 nc.scalar.activation(res[:], acc[:], EXP, scale=0.015625)
@@ -188,75 +180,110 @@ def tile_list_kvt_no_exp_kernel(
         nc.gpsimd.memset(warm_in[:], 0.0)
         nc.scalar.activation(warm_out[:], warm_in[:], EXP)
 
-        planes_01 = place_scales("planes_01", gather_scales("rows_01", 0, 2 * CH)[:].bitcast(I32), 2 * CH)
+        rows_0 = sbuf("rows_0", [P, 2 * CH], U8)
+        gather_scales(rows_0[:], 0)
+        planes = [place_scales(plane_tiles[0], rows_0)]
         wk_s, wq_s = w_scales[:, 0], w_scales[:, 1]
-        deal(nc.gpsimd, wk_s[0:100], wks_raw[0:100], 2)
-        x_raw = sbuf("x_raw", [P, 2, 4, M], F32)
-        nc.sync.dma_start(x_raw[:], x.rearrange("(a p i) m -> p a i m", a=2, i=4))
-        planes_23 = place_scales("planes_23", gather_scales("rows_23", 2 * CH, J)[:].bitcast(I32), 2 * CH)
+        for q in range(4):
+            deal(nc.scalar.copy, wk_s[32 * q : 32 * q + 4].bitcast(U32), wks_raw[q].bitcast(U32), 2)
+        wqs_raw = sbuf("wqs_raw", [P, 2, R // 4], I32)
+        nc.vector.memset(wqs_raw[:], 0)
+        rows_1 = sbuf("rows_1", [P, 2 * CH], U8)
+        for half in range(2):
+            gather_scales(rows_1[:, half * CH : (half + 1) * CH], (2 + half) * CH)
+        x_rows = x.rearrange("(a p i) m -> a p i m", a=2, i=4)
+        x_raw = [sbuf("x%d_raw" % a, [P, 4, M], F32) for a in range(2)]
+        for a in range(2):
+            nc.sync.dma_start(x_raw[a][:], x_rows[a])
+        for q in range(4):
+            load_scale_rows(wqs_raw[32 * q : 32 * q + 4], wq_scales, q)
         wq_raw = sbuf("wq_raw", [P, 2, R], I32)
         nc.sync.dma_start(wq_raw[:], wq_words.rearrange("a p r i -> p a (r i)").bitcast(I32))
-        wqs_raw = sbuf("wqs_raw", [P, 2, R // 4], I32)
-        nc.gpsimd.memset(wqs_raw[:], 0)
-        for q in range(4):
-            load_scale_rows(wqs_raw, wq_scales, q, nc.sync)
+        planes.append(place_scales(plane_tiles[1], rows_1))
 
-        warm = psum.tile([P, CH], F32, name="warm", tag="warm", offset=(KEY_BANKS + SCORE_BANKS - 1) * BANK)
+        warm = psum.tile([P, CH], F32, name="warm", tag="warm", offset=(BANKS - 1) * BANK)
         for i in range(4):
             nc.tensor.matmul_mx(
-                warm[:], lhsT=tab_w[:, 0 : P // 2].bitcast(FP4X4), lhsT_scale=tab_s[:, 0:P],
-                rhs=tab_w[:, 0 : CH // 2].bitcast(FP4X4), rhs_scale=tab_s[:, 0:CH], start=True, stop=True,
+                warm[:], lhsT=rows_0[:, 0 : 2 * P].bitcast(FP4X4), lhsT_scale=rows_1[:, 0:P],
+                rhs=rows_0[:].bitcast(FP4X4), rhs_scale=rows_1[:, 0:CH], start=True, stop=True,
             )
 
-        both_012 = sbuf("both_012", [P, 3 * CH - NB], U32)
-        both_0 = gather_words(0, both_012[:, 2 * CH - NB :])
-        wk = sbuf("wk", [P, 4, 2, 64], I32)
-        deal(nc.gpsimd, wk[:], wk_raw[:], 4)
-        parted0 = part_words(0, both_0, 0, [NB, 3 * NB])
-        kb0 = keys(0, parted0, planes_01, 0, nc.scalar.copy)
-        both_12 = gather_words(1, both_012[:, 0 : 2 * CH])
-        parted1 = part_words(1, both_12[:, 0:CH], 0, [CH])
-        kb1 = keys(4, parted1, planes_01, CH, nc.scalar.copy)
-
-        parted2 = part_words(2, both_12[:, CH:], 0, [3 * NB])
-        kb2 = sbuf("kb2", [P, CH, 4], BF16)
-        keys_into(kb2[:, 0 : 3 * NB], 8, parted2, planes_23, 0, nc.scalar.copy)
+        kb = [sbuf("kb%d" % c, [P, width, 4], BF16) for c, width in enumerate([CH, UNIT, CH])]
         xb = sbuf("xb", [P, 2, M, 4], BF16)
-        for a, copy in enumerate([nc.scalar.copy, nc.vector.tensor_copy]):
+
+        def cast_x(a, copy):
             copy(
                 xb[:, a].rearrange("p (c j) i -> p c i j", j=4),
-                x_raw[:, a].rearrange("p i (c j) -> p c i j", j=4),
+                x_raw[a][:].rearrange("p i (c j) -> p c i j", j=4),
             )
-        wq = sbuf("wq", [P, 4, 2, 128], I32)
-        deal(nc.gpsimd, wq[:], wq_raw[:], 8)
+
+        both_0 = sbuf("both_0", [P, 2 * UNIT - 16], U32)
+        gather_words(0, both_0[:, UNIT - 16 :])
+        wk = sbuf("wk", [P, 4, 2, 64], I32)
+        for half in range(2):
+            slots = slice(2 * half, 2 * half + 2)
+            nc.scalar.copy(
+                wk[:, slots].bitcast(U32).rearrange("p t a (b w) -> p t (a b) w", w=4),
+                wk_raw[:].bitcast(U32).rearrange("p a (b t w) -> p t (a b) w", t=4, w=4)[:, slots],
+            )
+        part_words(both_0[:, UNIT - 16 : UNIT + NB - 16])
+        part_words(both_0[:, UNIT + NB - 16 :])
+        gather_words(UNIT, both_0[:, 0:UNIT])
+        both_1 = sbuf("both_1", [P, CH], U32)
+        gather_words(2 * UNIT, both_1[:, 0:UNIT])
+        part_words(both_0[:, 0:UNIT])
+        gather_words(3 * UNIT, both_1[:, UNIT:])
+        part_words(both_1[:, 0:UNIT])
+        part_words(both_1[:, UNIT:])
+        cast_x(0, nc.scalar.copy)
+        keys(range(6), nc.scalar.copy)
+        waiting = [key_bank(b) for b in (6, 7)]
+        cast_x(1, nc.vector.tensor_copy)
+        deal(nc.vector.tensor_copy, wq_s[0:100], wqs_raw[0:100], 2)
         x_codes, x_scales = quantise("x", xb[:].rearrange("p a m i -> p (a m i)"), 2 * M)
-        deal(nc.gpsimd, wq_s[0:100], wqs_raw[0:100], 2)
+        wq = sbuf("wq", [P, 4, 2, 128], I32)
+        deal(nc.vector.tensor_copy, wq[:], wq_raw[:], 8)
+        both_2 = sbuf("both_2", [P, CH], U32)
+        gather_words(4 * UNIT, both_2[:, 0:UNIT])
+        k0 = quantise_keys("k0", kb[0])
+        part_words(both_2[:, 0:UNIT])
+        gather_words(5 * UNIT, both_2[:, UNIT:])
         qb = sbuf("qb", [P, M, 4], BF16)
         for h in range(M // NB):
-            project(
-                11 + h, nc.scalar.copy, qb[:, h * NB : (h + 1) * NB, :], wq, wq_s, FP8X4,
+            bank = project(
+                wq, wq_s, FP8X4,
                 [x_codes[:, a * M + h * NB : a * M + (h + 1) * NB].bitcast(FP8X4) for a in range(2)],
                 [x_scales[:, a * M + h * NB : a * M + (h + 1) * NB] for a in range(2)],
             )
-        parted2 = part_words(2, both_12[:, CH:], 3 * NB, [NB])
-        keys_into(kb2[:, 3 * NB :], 13, parted2, planes_23, 3 * NB, nc.scalar.copy)
-        both_3 = gather_words(3, sbuf("both_3", [P, CH], U32)[:])
-        k0 = quantise_keys("k0", kb0, CH)
-        q_codes, q_scales = quantise("q", qb[:].rearrange("p m t -> p (m t)"), M)
+            nc.scalar.copy(qb[:, h * NB : (h + 1) * NB, :], bank)
+        kb1_late = sbuf("kb1_late", [P, UNIT, 4], BF16)
+        for i, bank in enumerate(waiting):
+            nc.scalar.copy(kb1_late[:, i * NB : (i + 1) * NB, :], bank)
+        q_codes, q_scales = quantise_keys("q", qb)
+        part_words(both_2[:, UNIT:])
+        waiting = [key_bank(b) for b in (8, 9)]
         chunk_scores(0, k0)
-        parted3 = part_words(3, both_3, 0, [NB, 3 * NB])
-        k1 = quantise_keys("k1", kb1, CH)
-        k2 = quantise_keys("k2", kb2, CH)
-        kb3 = [sbuf("kb_14", [P, UNIT, 4], BF16)]
-        keys_into(kb3[0][:, 0:NB], 14, parted3[:1], planes_23, CH, nc.vector.tensor_copy)
+        for b, bank in zip((8, 9), waiting):
+            nc.scalar.copy(key_columns(b), bank)
+        keys([10, 11], nc.scalar.copy)
+        both_3 = sbuf("both_3", [P, CH], U32)
+        gather_words(6 * UNIT, both_3[:])
+        k1 = [sbuf("k1_codes", [P, CH], U32), sbuf("k1_scales", [P, CH], U8)]
+        for i, src in enumerate([kb[1], kb1_late]):
+            half = slice(i * UNIT, (i + 1) * UNIT)
+            nc.vector.quantize_mx(k1[0][:, half].bitcast(FP8X4), k1[1][:, half], src[:].rearrange("p n t -> p (n t)"))
+            part_words(both_3[:, half])
+        units = [sbuf("unit%d" % u, [P, width, 4], BF16) for u, width in enumerate([UNIT, NB, NB])]
+        nc.vector.tensor_copy(units[0][:, 0:NB], key_bank(12))
         chunk_scores(1, k1)
-        keys_into(kb3[0][:, NB:], 15, parted3[1:2], planes_23, CH + NB, nc.vector.tensor_copy)
-        kb3.append(keys(16, parted3[2:3], planes_23, CH + 2 * NB, nc.vector.tensor_copy))
+        k2 = quantise_keys("k2", kb[2])
+        nc.vector.tensor_copy(units[0][:, NB:], key_bank(13))
+        nc.vector.tensor_copy(units[1][:], key_bank(14))
         chunk_scores(2, k2)
-        kb3.append(keys(17, parted3[3:], planes_23, CH + 3 * NB, nc.vector.tensor_copy))
+        nc.vector.tensor_copy(units[2][:], key_bank(15))
         j0 = 3 * CH
-        for u, kb in enumerate(kb3):
-            width = kb.shape[1]
-            codes, scales = quantise_keys("k%d" % (3 + u), kb, width)
+        for u, unit in enumerate(units):
+            width = unit.shape[1]
+            codes, scales = quantise_keys("k%d" % (3 + u), unit)
             scores(6 + u, j0, width, codes[:], scales[:], nc.scalar if u == 2 else nc.sync)
             j0 = j0 + width

@@ -22,11 +22,13 @@ UNIT = 256
 BANKS = 8
 PLACES = {
     "x0_raw": 0, "wks_raw0": 4032, "wqs_raw": 4096, "x1_raw": 6016,
-    "wq_raw": 10112, "both_2": 10112, "k0_codes": 12160, "wks_raw1": 14144, "rows_1": 14208,
+    "wq_raw": 10112, "both_2": 10112, "k0_codes": 12288, "wks_raw1": 14144, "rows_1": 14208,
     "wk_raw": 16384, "both_1": 16384,
-    "qb": 20480, "k1_codes": 18496, "parted_10": 20544, "both_3": 22464,
-    "x_codes": 24576, "kb1_late": 26560,
+    "qb": 20480, "k1_codes": 18688, "parted_10": 20736, "both_3": 22464,
+    "x_codes": 24576, "kb1_late": 26368,
+    "parted_0": 28672, "xb": 28928,
 }
+ALIGN = {"x_codes": 256}
 BANK = 2048
 
 
@@ -41,8 +43,8 @@ def tile_list_kvt_no_exp_kernel(
 
         def sbuf(name, shape, dtype):
             if name in PLACES:
-                return reuse.tile(shape, dtype, name=name, tag=name, align_bytes=64, offset=PLACES[name])
-            return held.tile(shape, dtype, name=name, tag=name, align_bytes=64)
+                return reuse.tile(shape, dtype, name=name, tag=name, align_bytes=ALIGN.get(name, 64), offset=PLACES[name])
+            return held.tile(shape, dtype, name=name, tag=name, align_bytes=256)
 
         def load_scale_rows(raw, dram, q):
             nc.sync.dma_start(raw, dram[:, 4 * q : 4 * q + 4, :].rearrange("a r n -> r a n").bitcast(I32))
@@ -187,7 +189,7 @@ def tile_list_kvt_no_exp_kernel(
         for q in range(4):
             deal(nc.scalar.copy, wk_s[32 * q : 32 * q + 4].bitcast(U32), wks_raw[q].bitcast(U32), 2)
         wqs_raw = sbuf("wqs_raw", [P, 2, R // 4], I32)
-        nc.vector.memset(wqs_raw[:], 0)
+        nc.gpsimd.memset(wqs_raw[:], 0)
         rows_1 = sbuf("rows_1", [P, 2 * CH], U8)
         for half in range(2):
             gather_scales(rows_1[:, half * CH : (half + 1) * CH], (2 + half) * CH)
@@ -209,7 +211,6 @@ def tile_list_kvt_no_exp_kernel(
             )
 
         kb = [sbuf("kb%d" % c, [P, width, 4], BF16) for c, width in enumerate([CH, UNIT, CH])]
-        xb = sbuf("xb", [P, 2, M, 4], BF16)
 
         def cast_x(a, copy):
             copy(
@@ -235,8 +236,10 @@ def tile_list_kvt_no_exp_kernel(
         gather_words(3 * UNIT, both_1[:, UNIT:])
         part_words(both_1[:, 0:UNIT])
         part_words(both_1[:, UNIT:])
+        xb = sbuf("xb", [P, 2, M, 4], BF16)
+        keys(range(2), nc.scalar.copy)
         cast_x(0, nc.scalar.copy)
-        keys(range(6), nc.scalar.copy)
+        keys(range(2, 6), nc.scalar.copy)
         waiting = [key_bank(b) for b in (6, 7)]
         cast_x(1, nc.vector.tensor_copy)
         deal(nc.vector.tensor_copy, wq_s[0:100], wqs_raw[0:100], 2)
@@ -261,29 +264,35 @@ def tile_list_kvt_no_exp_kernel(
             nc.scalar.copy(kb1_late[:, i * NB : (i + 1) * NB, :], bank)
         q_codes, q_scales = quantise_keys("q", qb)
         part_words(both_2[:, UNIT:])
-        waiting = [key_bank(b) for b in (8, 9)]
+        keys([8], nc.scalar.copy)
+        waiting = key_bank(9)
         chunk_scores(0, k0)
-        for b, bank in zip((8, 9), waiting):
-            nc.scalar.copy(key_columns(b), bank)
+        nc.scalar.copy(key_columns(9), waiting)
         keys([10, 11], nc.scalar.copy)
         both_3 = sbuf("both_3", [P, CH], U32)
         gather_words(6 * UNIT, both_3[:])
         k1 = [sbuf("k1_codes", [P, CH], U32), sbuf("k1_scales", [P, CH], U8)]
-        for i, src in enumerate([kb[1], kb1_late]):
+
+        def quantise_half(i, src):
             half = slice(i * UNIT, (i + 1) * UNIT)
             nc.vector.quantize_mx(k1[0][:, half].bitcast(FP8X4), k1[1][:, half], src[:].rearrange("p n t -> p (n t)"))
-            part_words(both_3[:, half])
+
+        quantise_half(0, kb[1])
+        part_words(both_3[:, 0:UNIT])
+        part_words(both_3[:, UNIT:])
+        quantise_half(1, kb1_late)
         units = [sbuf("unit%d" % u, [P, width, 4], BF16) for u, width in enumerate([UNIT, NB, NB])]
-        nc.vector.tensor_copy(units[0][:, 0:NB], key_bank(12))
+        nc.scalar.copy(units[0][:, 0:NB], key_bank(12))
+        nc.vector.tensor_copy(units[0][:, NB:], key_bank(13))
         chunk_scores(1, k1)
         k2 = quantise_keys("k2", kb[2])
-        nc.vector.tensor_copy(units[0][:, NB:], key_bank(13))
+        k3 = quantise_keys("k3", units[0])
         nc.vector.tensor_copy(units[1][:], key_bank(14))
+        waiting = key_bank(15)
         chunk_scores(2, k2)
-        nc.vector.tensor_copy(units[2][:], key_bank(15))
-        j0 = 3 * CH
-        for u, unit in enumerate(units):
-            width = unit.shape[1]
-            codes, scales = quantise_keys("k%d" % (3 + u), unit)
-            scores(6 + u, j0, width, codes[:], scales[:], nc.scalar if u == 2 else nc.sync)
-            j0 = j0 + width
+        scores(6, 3 * CH, UNIT, k3[0][:], k3[1][:], nc.sync)
+        k4 = quantise_keys("k4", units[1])
+        nc.vector.tensor_copy(units[2][:], waiting)
+        scores(7, 3 * CH + UNIT, NB, k4[0][:], k4[1][:], nc.sync)
+        k5 = quantise_keys("k5", units[2])
+        scores(8, 3 * CH + UNIT + NB, NB, k5[0][:], k5[1][:], nc.scalar)

@@ -203,13 +203,6 @@ def tile_list_kvt_no_exp_kernel(
         nc.sync.dma_start(wq_raw[:], wq_words.rearrange("a p r i -> p a (r i)").bitcast(I32))
         planes.append(place_scales(plane_tiles[1], rows_1))
 
-        warm = psum.tile([P, CH], F32, name="warm", tag="warm", offset=(BANKS - 1) * BANK)
-        for i in range(4):
-            nc.tensor.matmul_mx(
-                warm[:], lhsT=rows_0[:, 0 : 2 * P].bitcast(FP4X4), lhsT_scale=rows_1[:, 0:P],
-                rhs=rows_0[:].bitcast(FP4X4), rhs_scale=rows_1[:, 0:CH], start=True, stop=True,
-            )
-
         kb = [sbuf("kb%d" % c, [P, width, 4], BF16) for c, width in enumerate([CH, UNIT, CH])]
 
         def cast_x(a, copy):

@@ -188,6 +188,14 @@ def tile_list_kvt_no_exp_kernel(
         wk_s, wq_s = w_scales[:, 0], w_scales[:, 1]
         for q in range(4):
             deal(nc.scalar.copy, wk_s[32 * q : 32 * q + 4].bitcast(U32), wks_raw[q].bitcast(U32), 2)
+        idle = psum.tile([P, CH], F32, name="idle", tag="idle", offset=(BANKS - 1) * BANK)
+        wk_codes = wk_raw[:].rearrange("p a n -> p (a n)")
+        wk_planes = wk_s.rearrange("p t a w -> p (t a w)").bitcast(U8)
+        for n in range(2):
+            nc.tensor.matmul_mx(
+                idle[:], lhsT=wk_codes[:, 0:64].bitcast(FP4X4), lhsT_scale=wk_planes[:, 0:P],
+                rhs=wk_codes[:, 0:256].bitcast(FP4X4), rhs_scale=wk_planes[:, 0:CH], start=True, stop=True,
+            )
         wqs_raw = sbuf("wqs_raw", [P, 2, R // 4], I32)
         nc.gpsimd.memset(wqs_raw[:], 0)
         rows_1 = sbuf("rows_1", [P, 2 * CH], U8)

@@ -22,9 +22,9 @@ UNIT = 256
 BANKS = 8
 PLACES = {
     "x0_raw": 0, "wks_raw0": 4032, "wqs_raw": 4096, "x1_raw": 6016,
-    "wq_raw": 10112, "both_2": 10112, "k0_codes": 12288, "wks_raw1": 14144, "rows_1": 14208,
+    "wq_raw": 10112, "both_2": 8192, "k0_codes": 10240, "k1_codes": 12288, "wks_raw1": 14144, "rows_1": 14208,
     "wk_raw": 16384, "both_1": 16384,
-    "qb": 20480, "k1_codes": 18688, "parted_10": 20736, "both_3": 22464,
+    "qb": 20480,  "both_3": 22464,
     "x_codes": 24576, "kb1_late": 26368,
     "parted_0": 28672, "xb": 28928,
 }
@@ -250,8 +250,16 @@ def tile_list_kvt_no_exp_kernel(
         both_2 = sbuf("both_2", [P, CH], U32)
         gather_words(4 * UNIT, both_2[:, 0:UNIT])
         k0 = quantise_keys("k0", kb[0])
-        part_words(both_2[:, 0:UNIT])
         gather_words(5 * UNIT, both_2[:, UNIT:])
+        part_words(both_2[:, 0:UNIT])
+        part_words(both_2[:, UNIT:])
+        k1 = [sbuf("k1_codes", [P, CH], U32), sbuf("k1_scales", [P, CH], U8)]
+
+        def quantise_half(i, src):
+            half = slice(i * UNIT, (i + 1) * UNIT)
+            nc.vector.quantize_mx(k1[0][:, half].bitcast(FP8X4), k1[1][:, half], src[:].rearrange("p n t -> p (n t)"))
+
+        quantise_half(0, kb[1])
         qb = sbuf("qb", [P, M, 4], BF16)
         for h in range(M // NB):
             bank = project(
@@ -264,24 +272,18 @@ def tile_list_kvt_no_exp_kernel(
         for i, bank in enumerate(waiting):
             nc.scalar.copy(kb1_late[:, i * NB : (i + 1) * NB, :], bank)
         q_codes, q_scales = quantise_keys("q", qb)
-        part_words(both_2[:, UNIT:])
         keys([8], nc.scalar.copy)
-        waiting = key_bank(9)
+        waiting = {b: key_bank(b) for b in (9, 10)}
         chunk_scores(0, k0)
-        nc.scalar.copy(key_columns(9), waiting)
-        keys([10, 11], nc.scalar.copy)
+        for b, bank in waiting.items():
+            nc.scalar.copy(key_columns(b), bank)
+        waiting = key_bank(11)
         both_3 = sbuf("both_3", [P, CH], U32)
         gather_words(6 * UNIT, both_3[:])
-        k1 = [sbuf("k1_codes", [P, CH], U32), sbuf("k1_scales", [P, CH], U8)]
-
-        def quantise_half(i, src):
-            half = slice(i * UNIT, (i + 1) * UNIT)
-            nc.vector.quantize_mx(k1[0][:, half].bitcast(FP8X4), k1[1][:, half], src[:].rearrange("p n t -> p (n t)"))
-
-        quantise_half(0, kb[1])
+        quantise_half(1, kb1_late)
         part_words(both_3[:, 0:UNIT])
         part_words(both_3[:, UNIT:])
-        quantise_half(1, kb1_late)
+        nc.vector.tensor_copy(key_columns(11), waiting)
         units = [sbuf("unit%d" % u, [P, width, 4], BF16) for u, width in enumerate([UNIT, NB, NB])]
         nc.scalar.copy(units[0][:, 0:NB], key_bank(12))
         nc.vector.tensor_copy(units[0][:, NB:], key_bank(13))
@@ -289,8 +291,8 @@ def tile_list_kvt_no_exp_kernel(
         k2 = quantise_keys("k2", kb[2])
         k3 = quantise_keys("k3", units[0])
         nc.vector.tensor_copy(units[1][:], key_bank(14))
-        waiting = key_bank(15)
         chunk_scores(2, k2)
+        waiting = key_bank(15)
         scores(6, 3 * CH, UNIT, k3[0][:], k3[1][:], nc.sync)
         k4 = quantise_keys("k4", units[1])
         nc.vector.tensor_copy(units[2][:], waiting)

@@ -121,7 +121,7 @@ def tile_list_kvt_no_exp_kernel(
                         start=(a == 0),
                         stop=(a == 1),
                     )
-            return bank[:].rearrange("p t n -> p n t")
+            return bank[:].rearrange("p t (c j) -> p c t j", j=2)
 
         def key_bank(b):
             n0 = (b % 8) * NB
@@ -131,8 +131,11 @@ def tile_list_kvt_no_exp_kernel(
                 [planes[b // 8][a][:, n0 : n0 + NB] for a in range(2)],
             )
 
+        def in_pairs(columns):
+            return columns.rearrange("p (c j) t -> p c t j", j=2)
+
         def key_columns(b):
-            return kb[b // 4][:, (b % 4) * NB : (b % 4 + 1) * NB, :]
+            return in_pairs(kb[b // 4][:, (b % 4) * NB : (b % 4 + 1) * NB, :])
 
         def keys(banks, copy):
             for b in banks:
@@ -267,10 +270,10 @@ def tile_list_kvt_no_exp_kernel(
                 [x_codes[:, a * M + h * NB : a * M + (h + 1) * NB].bitcast(FP8X4) for a in range(2)],
                 [x_scales[:, a * M + h * NB : a * M + (h + 1) * NB] for a in range(2)],
             )
-            nc.scalar.copy(qb[:, h * NB : (h + 1) * NB, :], bank)
+            nc.scalar.copy(in_pairs(qb[:, h * NB : (h + 1) * NB, :]), bank)
         kb1_late = sbuf("kb1_late", [P, UNIT, 4], BF16)
         for i, bank in enumerate(waiting):
-            nc.scalar.copy(kb1_late[:, i * NB : (i + 1) * NB, :], bank)
+            nc.scalar.copy(in_pairs(kb1_late[:, i * NB : (i + 1) * NB, :]), bank)
         q_codes, q_scales = quantise_keys("q", qb)
         keys([8], nc.scalar.copy)
         waiting = {b: key_bank(b) for b in (9, 10)}
@@ -285,17 +288,17 @@ def tile_list_kvt_no_exp_kernel(
         part_words(both_3[:, UNIT:])
         nc.vector.tensor_copy(key_columns(11), waiting)
         units = [sbuf("unit%d" % u, [P, width, 4], BF16) for u, width in enumerate([UNIT, NB, NB])]
-        nc.scalar.copy(units[0][:, 0:NB], key_bank(12))
-        nc.vector.tensor_copy(units[0][:, NB:], key_bank(13))
+        nc.scalar.copy(in_pairs(units[0][:, 0:NB]), key_bank(12))
+        nc.vector.tensor_copy(in_pairs(units[0][:, NB:]), key_bank(13))
         chunk_scores(1, k1)
         k2 = quantise_keys("k2", kb[2])
         k3 = quantise_keys("k3", units[0])
-        nc.vector.tensor_copy(units[1][:], key_bank(14))
+        nc.vector.tensor_copy(in_pairs(units[1][:]), key_bank(14))
         chunk_scores(2, k2)
         waiting = key_bank(15)
         scores(6, 3 * CH, UNIT, k3[0][:], k3[1][:], nc.sync)
         k4 = quantise_keys("k4", units[1])
-        nc.vector.tensor_copy(units[2][:], waiting)
+        nc.vector.tensor_copy(in_pairs(units[2][:]), waiting)
         scores(7, 3 * CH + UNIT, NB, k4[0][:], k4[1][:], nc.sync)
         k5 = quantise_keys("k5", units[2])
         scores(8, 3 * CH + UNIT + NB, NB, k5[0][:], k5[1][:], nc.scalar)

@@ -22,9 +22,9 @@ UNIT = 256
 BANKS = 8
 PLACES = {
     "x0_raw": 0, "wks_raw0": 4032, "wqs_raw": 4096, "x1_raw": 6016,
-    "wq_raw": 10112, "both_2": 8192, "k0_codes": 10240, "k1_codes": 12288, "wks_raw1": 14144, "rows_1": 14208,
+    "wq_raw": 10112, "both_2": 7232, "k0_codes": 10240, "k1_codes": 12288, "wks_raw1": 14144, "rows_1": 14208,
     "wk_raw": 16384, "both_1": 16384,
-    "qb": 20480,  "both_3": 22464,
+    "qb": 20480, "parted_12": 20480, "both_3": 22464,
     "x_codes": 24576, "kb1_late": 26368,
     "parted_0": 28672, "xb": 28928,
 }
@@ -250,19 +250,20 @@ def tile_list_kvt_no_exp_kernel(
         x_codes, x_scales = quantise("x", xb[:].rearrange("p a m i -> p (a m i)"), 2 * M)
         wq = sbuf("wq", [P, 4, 2, 128], I32)
         deal(nc.vector.tensor_copy, wq[:], wq_raw[:], 8)
-        both_2 = sbuf("both_2", [P, CH], U32)
-        gather_words(4 * UNIT, both_2[:, 0:UNIT])
-        k0 = quantise_keys("k0", kb[0])
-        gather_words(5 * UNIT, both_2[:, UNIT:])
-        part_words(both_2[:, 0:UNIT])
-        part_words(both_2[:, UNIT:])
         k1 = [sbuf("k1_codes", [P, CH], U32), sbuf("k1_scales", [P, CH], U8)]
 
         def quantise_half(i, src):
             half = slice(i * UNIT, (i + 1) * UNIT)
             nc.vector.quantize_mx(k1[0][:, half].bitcast(FP8X4), k1[1][:, half], src[:].rearrange("p n t -> p (n t)"))
 
+        both_2 = sbuf("both_2", [P, 3 * UNIT - 16], U32)
+        gather_words(4 * UNIT, both_2[:, UNIT - 16 : 2 * UNIT - 16])
+        k0 = quantise_keys("k0", kb[0])
+        part_words(both_2[:, UNIT - 16 : 2 * UNIT - 16])
+        gather_words(5 * UNIT, both_2[:, 2 * UNIT - 16 :])
         quantise_half(0, kb[1])
+        part_words(both_2[:, 2 * UNIT - 16 :])
+        gather_words(6 * UNIT, both_2[:, 0:UNIT])
         qb = sbuf("qb", [P, M, 4], BF16)
         for h in range(M // NB):
             bank = project(
@@ -281,15 +282,15 @@ def tile_list_kvt_no_exp_kernel(
         for b, bank in waiting.items():
             nc.scalar.copy(key_columns(b), bank)
         waiting = key_bank(11)
-        both_3 = sbuf("both_3", [P, CH], U32)
-        gather_words(6 * UNIT, both_3[:])
+        part_words(both_2[:, 0:UNIT])
+        both_3 = sbuf("both_3", [P, UNIT], U32)
+        gather_words(7 * UNIT, both_3[:])
         quantise_half(1, kb1_late)
-        part_words(both_3[:, 0:UNIT])
-        part_words(both_3[:, UNIT:])
+        part_words(both_3[:])
         nc.vector.tensor_copy(key_columns(11), waiting)
         units = [sbuf("unit%d" % u, [P, width, 4], BF16) for u, width in enumerate([UNIT, NB, NB])]
         nc.scalar.copy(in_pairs(units[0][:, 0:NB]), key_bank(12))
-        nc.vector.tensor_copy(in_pairs(units[0][:, NB:]), key_bank(13))
+        nc.scalar.copy(in_pairs(units[0][:, NB:]), key_bank(13))
         chunk_scores(1, k1)
         k2 = quantise_keys("k2", kb[2])
         k3 = quantise_keys("k3", units[0])

from contextlib import ExitStack

import concourse.mybir as mybir

K, R, M, T, J = 1024, 512, 256, 4096, 2048
FLOPS = 2 * K * R * M + 2 * K * R * J + 2 * R * M * J

F32 = mybir.dt.float32
BF16 = mybir.dt.bfloat16
I32 = mybir.dt.int32
U32 = mybir.dt.uint32
U16 = mybir.dt.uint16
U8 = mybir.dt.uint8
FP8X4 = mybir.dt.float8_e4m3fn_x4
FP4X4 = mybir.dt.float4_e2m1fn_x4
EXP = mybir.ActivationFunctionType.Exp

P = 128
CH = 512
NB = 128
UNIT = 256
BANKS = 8
PLACES = {
    "x0_raw": 0, "wks_raw0": 4032, "wqs_raw": 4096, "x1_raw": 6016,
    "wq_raw": 10112, "both_2": 7232, "k0_codes": 10240, "k1_codes": 12288, "wks_raw1": 14144, "rows_1": 14208,
    "wk_raw": 16384, "both_1": 16384,
    "qb": 20480, "parted_12": 20480, "both_3": 22464,
    "x_codes": 24576, "kb1_late": 26368,
    "parted_0": 28672, "xb": 28928,
}
ALIGN = {"x_codes": 256}
BANK = 2048


def tile_list_kvt_no_exp_kernel(
    tc, tab_words, tab_scales, x, wq_words, wq_scales, wk_words, wk_scales, offs, out
):
    nc = tc.nc
    with ExitStack() as ctx:
        held = ctx.enter_context(tc.tile_pool(name="held", bufs=1))
        reuse = ctx.enter_context(tc.tile_pool(name="reuse", bufs=1))
        psum = ctx.enter_context(tc.psum_pool(name="psum", bufs=1))

        def sbuf(name, shape, dtype):
            if name in PLACES:
                return reuse.tile(shape, dtype, name=name, tag=name, align_bytes=ALIGN.get(name, 64), offset=PLACES[name])
            return held.tile(shape, dtype, name=name, tag=name, align_bytes=256)

        def load_scale_rows(raw, dram, q):
            nc.sync.dma_start(raw, dram[:, 4 * q : 4 * q + 4, :].rearrange("a r n -> r a n").bitcast(I32))

        offsets = held.tile([P, J // 16], U16, name="offsets")
        nc.sync.dma_start(offsets[:], offs)
        tab_s = sbuf("tab_s", [P, T], U8)
        nc.sync.dma_start(tab_s[96:P, :].bitcast(I32), tab_scales.rearrange("a s t -> s a t").bitcast(I32))
        wks_tiles = [sbuf("wks_raw%d" % u, [P, 2, 2, R // 4], I32) for u in range(2)]
        wks_raw = [wks_tiles[q // 2][32 * q : 32 * q + 4, q % 2] for q in range(4)]
        for q in range(4):
            load_scale_rows(wks_raw[q], wk_scales, q)
        tab_w = sbuf("tab_w", [P, T], I32)
        nc.sync.dma_start(tab_w[:], tab_words[0].rearrange("p t b -> p (t b)").bitcast(I32))
        wk_raw = sbuf("wk_raw", [P, 2, R // 2], I32)
        nc.sync.dma_start(wk_raw[:], wk_words.rearrange("a p n -> p a n").bitcast(I32))

        def cleared_planes(g):
            planes = sbuf("planes_%d" % g, [P, 2, 2 * CH], U8)
            nc.gpsimd.memset(planes[:].rearrange("p a n -> p (a n)").bitcast(I32), 0)
            return planes

        nc.vector.memset(tab_s[0:96, :].bitcast(I32), 0)
        w_scales = sbuf("w_scales", [P, 2, 4, 2, 32], I32)
        nc.gpsimd.memset(w_scales[:], 0)
        plane_tiles = [cleared_planes(g) for g in range(2)]

        def deal(copy, dealt, raw, run):
            copy(
                dealt.rearrange("p t a (b w) -> p t (a b) w", w=run),
                raw.rearrange("p a (b t w) -> p t (a b) w", t=4, w=run),
            )

        def gather_scales(rows, j0):
            nc.vector.tensor_copy(rows, tab_s[:].indirect(offsets[:, j0 // 16 : (j0 + rows.shape[1]) // 16]))

        def place_scales(planes, rows):
            for q in range(4):
                nc.sync.dma_start(
                    planes[32 * q : 32 * q + 4].bitcast(I32), rows[96 + 8 * q : 104 + 8 * q, :].bitcast(I32)
                )
            return [planes[:, a, :] for a in range(2)]

        def gather_words(j0, both):
            columns = slice(j0 // 16, (j0 + both.shape[1]) // 16)
            nc.vector.tensor_copy(both, tab_w[:].bitcast(U32).indirect(offsets[:, columns]))

        parted = []

        def part_words(both):
            piece = both.shape[1]
            part = sbuf("parted_%d" % len(parted), [P, 2, piece], U16)
            nc.vector.tensor_copy(part[:], both.bitcast(U16).rearrange("p (n d) -> p d n", d=2))
            parted.extend(part[:, :, n : n + NB] for n in range(0, piece, NB))

        steps = []

        def next_bank(shape):
            step = len(steps)
            steps.append(step)
            name = "bank%d" % step
            return psum.tile(shape, F32, name=name, tag=name, offset=(step % BANKS) * BANK)

        def project(w, w_s, w_dtype, rhs, rhs_s):
            bank = next_bank([P, 4, NB])
            for t in range(4):
                for a in range(2):
                    nc.tensor.matmul_mx(
                        bank[:, t, :],
                        lhsT=w[:, t, a, :].bitcast(w_dtype),
                        lhsT_scale=w_s[:, t, a, :].bitcast(U8),
                        rhs=rhs[a],
                        rhs_scale=rhs_s[a],
                        start=(a == 0),
                        stop=(a == 1),
                    )
            return bank[:].rearrange("p t (c j) -> p c t j", j=2)

        def key_bank(b):
            n0 = (b % 8) * NB
            return project(
                wk, wk_s, FP4X4,
                [parted[b][:, a, :].bitcast(FP4X4) for a in range(2)],
                [planes[b // 8][a][:, n0 : n0 + NB] for a in range(2)],
            )

        def in_pairs(columns):
            return columns.rearrange("p (c j) t -> p c t j", j=2)

        def key_columns(b):
            return in_pairs(kb[b // 4][:, (b % 4) * NB : (b % 4 + 1) * NB, :])

        def keys(banks, copy):
            for b in banks:
                copy(key_columns(b), key_bank(b))

        def quantise(name, src, width):
            codes = sbuf(name + "_codes", [P, width], U32)
            scales = sbuf(name + "_scales", [P, width], U8)
            nc.vector.quantize_mx(codes[:].bitcast(FP8X4), scales[:], src)
            return codes, scales

        out_view = out.rearrange("(h p) j -> p h j", h=2)

        def quantise_keys(name, src):
            return quantise(name, src[:].rearrange("p n t -> p (n t)"), src.shape[1])

        def score_pass(acc, h, k_codes, k_scales):
            nc.tensor.matmul_mx(
                acc,
                lhsT=q_codes[:, h * P : (h + 1) * P].bitcast(FP8X4),
                lhsT_scale=q_scales[:, h * P : (h + 1) * P],
                rhs=k_codes.bitcast(FP8X4),
                rhs_scale=k_scales,
                start=True,
                stop=True,
            )

        def scores(u, j0, width, k_codes, k_scales, queue):
            acc = next_bank([P, 2, width])
            for h in range(2):
                score_pass(acc[:, h, :], h, k_codes, k_scales)
            res = sbuf("res_%d" % u, [P, 2, width], F32)
            nc.scalar.activation(res[:], acc[:], EXP, scale=0.015625)
            queue.dma_start(out_view[:, :, j0 : j0 + width], res[:])

        def chunk_scores(c, quantised):
            codes, scales = quantised
            for h in range(2):
                acc = next_bank([P, CH])
                score_pass(acc[:], h, codes[:], scales[:])
                res = sbuf("res_%d" % (2 * c + h), [P, CH], F32)
                nc.scalar.activation(res[:], acc[:], EXP, scale=0.015625)
                nc.sync.dma_start(out_view[:, h, c * CH : (c + 1) * CH], res[:])

        warm_in = sbuf("warm_in", [P, 1], F32)
        warm_out = sbuf("warm_out", [P, 1], F32)
        nc.gpsimd.memset(warm_in[:], 0.0)
        nc.scalar.activation(warm_out[:], warm_in[:], EXP)

        rows_0 = sbuf("rows_0", [P, 2 * CH], U8)
        gather_scales(rows_0[:], 0)
        planes = [place_scales(plane_tiles[0], rows_0)]
        wk_s, wq_s = w_scales[:, 0], w_scales[:, 1]
        for q in range(4):
            deal(nc.scalar.copy, wk_s[32 * q : 32 * q + 4].bitcast(U32), wks_raw[q].bitcast(U32), 2)
        idle = psum.tile([P, CH], F32, name="idle", tag="idle", offset=(BANKS - 1) * BANK)
        wk_codes = wk_raw[:].rearrange("p a n -> p (a n)")
        wk_planes = wk_s.rearrange("p t a w -> p (t a w)").bitcast(U8)
        for n in range(2):
            nc.tensor.matmul_mx(
                idle[:], lhsT=wk_codes[:, 0:64].bitcast(FP4X4), lhsT_scale=wk_planes[:, 0:P],
                rhs=wk_codes[:, 0:256].bitcast(FP4X4), rhs_scale=wk_planes[:, 0:CH], start=True, stop=True,
            )
        wqs_raw = sbuf("wqs_raw", [P, 2, R // 4], I32)
        nc.gpsimd.memset(wqs_raw[:], 0)
        rows_1 = sbuf("rows_1", [P, 2 * CH], U8)
        for half in range(2):
            gather_scales(rows_1[:, half * CH : (half + 1) * CH], (2 + half) * CH)
        x_rows = x.rearrange("(a p i) m -> a p i m", a=2, i=4)
        x_raw = [sbuf("x%d_raw" % a, [P, 4, M], F32) for a in range(2)]
        for a in range(2):
            nc.sync.dma_start(x_raw[a][:], x_rows[a])
        for q in range(4):
            load_scale_rows(wqs_raw[32 * q : 32 * q + 4], wq_scales, q)
        wq_raw = sbuf("wq_raw", [P, 2, R], I32)
        nc.sync.dma_start(wq_raw[:], wq_words.rearrange("a p r i -> p a (r i)").bitcast(I32))
        planes.append(place_scales(plane_tiles[1], rows_1))

        kb = [sbuf("kb%d" % c, [P, width, 4], BF16) for c, width in enumerate([CH, UNIT, CH])]

        def cast_x(a, copy):
            copy(
                xb[:, a].rearrange("p (c j) i -> p c i j", j=4),
                x_raw[a][:].rearrange("p i (c j) -> p c i j", j=4),
            )

        both_0 = sbuf("both_0", [P, 2 * UNIT - 16], U32)
        gather_words(0, both_0[:, UNIT - 16 :])
        wk = sbuf("wk", [P, 4, 2, 64], I32)
        for half in range(2):
            slots = slice(2 * half, 2 * half + 2)
            nc.scalar.copy(
                wk[:, slots].bitcast(U32).rearrange("p t a (b w) -> p t (a b) w", w=4),
                wk_raw[:].bitcast(U32).rearrange("p a (b t w) -> p t (a b) w", t=4, w=4)[:, slots],
            )
        part_words(both_0[:, UNIT - 16 : UNIT + NB - 16])
        part_words(both_0[:, UNIT + NB - 16 :])
        gather_words(UNIT, both_0[:, 0:UNIT])
        both_1 = sbuf("both_1", [P, CH], U32)
        gather_words(2 * UNIT, both_1[:, 0:UNIT])
        part_words(both_0[:, 0:UNIT])
        gather_words(3 * UNIT, both_1[:, UNIT:])
        part_words(both_1[:, 0:UNIT])
        part_words(both_1[:, UNIT:])
        xb = sbuf("xb", [P, 2, M, 4], BF16)
        keys(range(2), nc.scalar.copy)
        cast_x(0, nc.scalar.copy)
        keys(range(2, 6), nc.scalar.copy)
        waiting = [key_bank(b) for b in (6, 7)]
        cast_x(1, nc.vector.tensor_copy)
        deal(nc.vector.tensor_copy, wq_s[0:100], wqs_raw[0:100], 2)
        x_codes, x_scales = quantise("x", xb[:].rearrange("p a m i -> p (a m i)"), 2 * M)
        wq = sbuf("wq", [P, 4, 2, 128], I32)
        deal(nc.vector.tensor_copy, wq[:], wq_raw[:], 8)
        k1 = [sbuf("k1_codes", [P, CH], U32), sbuf("k1_scales", [P, CH], U8)]

        def quantise_half(i, src):
            half = slice(i * UNIT, (i + 1) * UNIT)
            nc.vector.quantize_mx(k1[0][:, half].bitcast(FP8X4), k1[1][:, half], src[:].rearrange("p n t -> p (n t)"))

        both_2 = sbuf("both_2", [P, 3 * UNIT - 16], U32)
        gather_words(4 * UNIT, both_2[:, UNIT - 16 : 2 * UNIT - 16])
        k0 = quantise_keys("k0", kb[0])
        part_words(both_2[:, UNIT - 16 : 2 * UNIT - 16])
        gather_words(5 * UNIT, both_2[:, 2 * UNIT - 16 :])
        quantise_half(0, kb[1])
        part_words(both_2[:, 2 * UNIT - 16 :])
        gather_words(6 * UNIT, both_2[:, 0:UNIT])
        qb = sbuf("qb", [P, M, 4], BF16)
        for h in range(M // NB):
            bank = project(
                wq, wq_s, FP8X4,
                [x_codes[:, a * M + h * NB : a * M + (h + 1) * NB].bitcast(FP8X4) for a in range(2)],
                [x_scales[:, a * M + h * NB : a * M + (h + 1) * NB] for a in range(2)],
            )
            nc.scalar.copy(in_pairs(qb[:, h * NB : (h + 1) * NB, :]), bank)
        kb1_late = sbuf("kb1_late", [P, UNIT, 4], BF16)
        for i, bank in enumerate(waiting):
            nc.scalar.copy(in_pairs(kb1_late[:, i * NB : (i + 1) * NB, :]), bank)
        q_codes, q_scales = quantise_keys("q", qb)
        keys([8], nc.scalar.copy)
        waiting = {b: key_bank(b) for b in (9, 10)}
        chunk_scores(0, k0)
        for b, bank in waiting.items():
            nc.scalar.copy(key_columns(b), bank)
        waiting = key_bank(11)
        part_words(both_2[:, 0:UNIT])
        both_3 = sbuf("both_3", [P, UNIT], U32)
        gather_words(7 * UNIT, both_3[:])
        quantise_half(1, kb1_late)
        part_words(both_3[:])
        nc.vector.tensor_copy(key_columns(11), waiting)
        units = [sbuf("unit%d" % u, [P, width, 4], BF16) for u, width in enumerate([UNIT, NB, NB])]
        nc.scalar.copy(in_pairs(units[0][:, 0:NB]), key_bank(12))
        nc.scalar.copy(in_pairs(units[0][:, NB:]), key_bank(13))
        chunk_scores(1, k1)
        k2 = quantise_keys("k2", kb[2])
        k3 = quantise_keys("k3", units[0])
        nc.vector.tensor_copy(in_pairs(units[1][:]), key_bank(14))
        chunk_scores(2, k2)
        waiting = key_bank(15)
        scores(6, 3 * CH, UNIT, k3[0][:], k3[1][:], nc.sync)
        k4 = quantise_keys("k4", units[1])
        nc.vector.tensor_copy(in_pairs(units[2][:]), waiting)
        scores(7, 3 * CH + UNIT, NB, k4[0][:], k4[1][:], nc.sync)
        k5 = quantise_keys("k5", units[2])
        scores(8, 3 * CH + UNIT + NB, NB, k5[0][:], k5[1][:], nc.scalar)
